import numpy as np, ml_dtypes
CORES = [6,15,38,47]
N = 4
import mx_ref
BF = ml_dtypes.bfloat16
def gcols(t, e):
    v = np.concatenate([t.reshape(8, 16, -1, 4), np.zeros((8, 16, 1, 4), BF)], axis=2)
    return np.ascontiguousarray(np.stack([v[g][:, e[g]] for g in range(8)])).reshape(128, -1)
def tile(rs):
    return np.stack(rs, axis=2).reshape(128, -1).astype(BF)
def pick(q, e):
    c = np.concatenate([q[0].reshape(128, -1, 4), np.zeros((128, 1, 4), np.uint8)], axis=1); s = np.concatenate([q[1], np.ones((16, 1), np.uint8)], axis=1)
    return (np.ascontiguousarray(c[:, e].reshape(128, -1)), np.ascontiguousarray(s[:, e]))
def join(*qs):
    return (np.concatenate([q[0] for q in qs], axis=1), np.concatenate([q[1] for q in qs], axis=1))
def put(q, e, v):
    c, s = q[0].reshape(128, -1, 4).copy(), q[1].copy(); c[:, e] = v[0].reshape(128, -1, 4); s[:, e] = v[1]
    return (c.reshape(128, -1), s)
def pk(c, s):
    return (np.ascontiguousarray(c), mx_ref.live(s))
def emit(q):
    return q[0], q[1]
def packed(v, rng):
    q = [mx_ref.quantize(np.ascontiguousarray(v[r])) for r in range(N)]
    return np.stack([a for a, b in q]), np.stack([mx_ref.plane(b, rng) for a, b in q])
def values_of_codes():
    e, c = np.zeros((128, 128, 4), np.float32), np.zeros((128, 2, 4), np.uint8)
    e[np.arange(128), np.arange(128), 0] = 1
    c[:127, :, 0] = np.arange(256).reshape(2, 128).T[:127]
    return mx_ref.matmul(mx_ref.quantize(e.reshape(128, 512).astype(BF)), (c.reshape(128, 8), np.full((16, 2), 127, np.uint8))).T.reshape(-1).astype(np.float64)
CODE_VALUE, SCALE_VALUE = values_of_codes(), 2.0 ** (np.arange(256) - 127.0)
def decode(q):
    return (CODE_VALUE[q[0]].reshape(16, 8, -1, 4) * SCALE_VALUE[q[1]][:, None, :, None] + 0.0).reshape(128, -1).astype(np.float32)
def f(rng, *shape):
    return mx_ref.flush((rng.standard_normal(shape, dtype=np.float32) * np.exp2(rng.integers(-2, 3, shape[:-1] + (1,)))).astype(BF))
def wide(rng, *shape, cols=0):
    v = rng.standard_normal(shape, dtype=np.float32) * np.exp2(rng.integers(-12, 13, shape)).astype(np.float32)
    if cols: v *= np.repeat(np.exp2(rng.integers(-cols, cols + 1, shape[:-2] + (1, shape[-1] // 4))) * (rng.random(shape[:-2] + (1, shape[-1] // 4)) > 0.0625), 4, axis=-1).astype(np.float32)
    return mx_ref.flush(v.astype(BF))
C, R = 384, 3
def order(p):
    return np.argsort(-(p[::16] + np.float32(0.0)), axis=1, kind="stable")
def clear(v):
    v = np.array(v)
    v[np.abs(v.astype(np.float32)) < np.float32(2.0 ** -16)] = 0
    return v
def numbers_of(rng):
    return {"x": clear(f(rng, N, 128, 4 * C)), "u": np.array(f(rng, N, 128, 512)), "v": np.array(f(rng, N, 128, 512))}
def weights(rng, w):
    c, p = packed(np.stack([w] * N), rng)
    return {"wc": c, "ws": p}
def aside(rng, k):
    w = np.array(f(rng, 128, 2048)).reshape(8, 16, 4, 8, 16, 4)
    w[:, :k] = 0
    w[:, :, :, :, 0] = 0
    w[:, :, :, :, 8:] = 0
    return weights(rng, w.reshape(128, 2048))
def signs(rng):
    return np.stack([rng.permutation(8) % 2 * 2.0 - 1.0 for r in range(N)])
def setup_inputs(rng):
    return {**numbers_of(rng), **weights(rng, f(rng, 128, 2048))}
def setup_inputs_ties(rng):
    d = numbers_of(rng)
    e = rng.permutation(N)
    x = d["x"].reshape(N, 8, 16, C, 4)
    for r in range(N):
        k = np.zeros(C, int) if r == e[0] else rng.permutation(C) % 3
        a = x[r][:, :8, :3].copy()
        a[:, :, 2] = 0
        x[r][:, :8] = a[:, :, k]
    x[e[1]] = 0
    u = d["u"].reshape(N, 8, 16, 128, 4)
    u[:, :, 8:, ::16] = 0
    w = np.array(f(rng, 128, 2048)).reshape(8, 16, 4, 8, 16, 4)
    w[:, 8:, :, :, :8] = 0
    return {"x": x.reshape(N, 128, 4 * C), "u": u.reshape(N, 128, 512), "v": d["v"], **weights(rng, w.reshape(128, 2048))}
def setup_inputs_near(rng):
    d = numbers_of(rng)
    x = d["x"].astype(np.float32).reshape(N, 8, 16, C, 4)
    s = (np.arange(C) // 2 + rng.integers(0, C // 2, (N, 8, 1))) % (C // 2)
    g = ((s[..., None] >> np.arange(8)) & 1) * np.exp2(np.arange(8) - 23.0)
    x[:, :, 0] = 0
    x[:, :, 0, :, 0] = signs(rng)[:, :, None]
    x[:, :, 8] = g[..., :4]
    x[:, :, 9] = g[..., 4:]
    x[:, :, 10:] = 0
    u = d["u"].reshape(N, 128, 128, 4)
    u[:, :, ::16] = 0
    k = np.where(rng.permutation(N) < N // 2, 2.0 ** -30, 1.0).astype(np.float32).astype(BF)
    for h in range(0, 128, 16):
        u[:, h, h, 0] = k
        u[:, h + 8:h + 10, h] = k[:, None, None]
    return {"x": x.reshape(N, 128, 4 * C).astype(BF), "u": u.reshape(N, 128, 512), "v": d["v"], **aside(rng, 0)}
def setup_inputs_huge(rng):
    d = numbers_of(rng)
    x = 2.0 ** 30 * (0.6 + 0.4 * rng.random((N, 128, C, 4)))
    c = np.stack([rng.permutation(C) % 2 * 2.0 - 1.0 for r in range(N)])
    c[rng.permutation(N) < N // 2] = 1
    x *= c[:, None, :, None]
    u = d["u"].reshape(N, 128, 128, 4)
    a = 2.0 ** 30 * (1 - 0.25 * rng.random((N, 128, 8, 4))) * signs(rng)[:, None, :, None]
    u[:, :, ::16] = a.astype(np.float32).astype(BF)
    w = np.zeros((128, 4, 128, 4), np.float32)
    i = np.arange(128)
    for b in range(4): w[i, b, i, b] = 16
    return {"x": x.astype(np.float32).reshape(N, 128, 4 * C).astype(BF), "u": u.reshape(N, 128, 512), "v": d["v"], **weights(rng, w.reshape(128, 2048).astype(BF))}
def setup_inputs_crowd(rng):
    d = numbers_of(rng)
    x = d["x"].astype(np.float32).reshape(N, 8, 16, C, 4)
    a, b = np.triu_indices(N, 1)
    k = rng.permutation(len(a))[(np.arange(C)[None, :] + np.arange(8)[:, None]) % len(a)]
    z = rng.integers(4, 8, (8, 8, C, 4)) * rng.choice([-1.0, 1.0], (8, 8, C, 4)) * 2.0 ** 26
    s = C - 1 - np.arange(C)
    digits = np.stack([s % 8, s // 8 % 8, s // 64, 0 * s], axis=1)
    for r in range(N):
        l = rng.integers(4, 8, (8, 8, C, 4)) * rng.choice([-1.0, 1.0], (8, 8, C, 4))
        l = np.where((a[k] == r)[:, None, :, None], z, np.where((b[k] == r)[:, None, :, None], -z, l))
        for g in range(8):
            o = rng.permutation(C)
            p = x[r, g]
            p[8:, o] = l[g]
            p[0, o] = digits
    u = d["u"].reshape(N, 128, 128, 4)
    u[:, :, ::16] = 0
    for h in range(0, 128, 16): u[:, h, h, :3] = np.array([1, 8, 64], np.float32).astype(BF)
    return {"x": x.reshape(N, 128, 4 * C).astype(BF), "u": u.reshape(N, 128, 512), "v": d["v"], **aside(rng, 8)}
def setup_inputs_spread(rng):
    d = setup_inputs(rng)
    d["x"] = clear(wide(rng, N, 128, 4 * C, cols=6))
    return d
def check_inputs(d):
    b = []
    for k in ("x", "u", "v"):
        a = np.abs(d[k].astype(np.float32))
        if not (np.isfinite(a).all() and ((a == 0) | (a >= 2.0 ** -30) & (a <= 2.0 ** 30)).all()): b.append("a value of " + k)
    if (d["wc"] != d["wc"][:1]).any(): b.append("wc differs between ranks")
    s = [mx_ref.live(p) for p in d["ws"]]
    if any((p != s[0]).any() for p in s): b.append("ws differs between ranks")
    if not (np.abs(decode(pk(d["wc"][0], d["ws"][0]))) <= 2.0 ** 30).all(): b.append("a number of W beyond 2**30")
    return b
def reference(x, u, v, wc, ws):
    w = pk(wc[0], ws[0])
    lay = [pick(w, np.arange(128 * b, 128 * b + 128)) for b in range(4)]
    qu = [mx_ref.quantize(u[r]) for r in range(N)]
    now = [x[r] for r in range(N)]
    for t in range(R):
        o = [order(mx_ref.matmul(qu[r], mx_ref.quantize(now[r]))) for r in range(N)]
        total = decode(mx_ref.quantize(gcols(now[0], o[0])))
        for r in range(1, N): total = total + decode(mx_ref.quantize(gcols(now[r], o[r])))
        m = mx_ref.quantize((total * np.float32(0.25)).astype(BF))
        h = mx_ref.quantize(tile([np.maximum(mx_ref.matmul(lay[b], m), np.float32(0.0)) * np.float32(0.0625) for b in range(4)]))
        back = decode(h).astype(BF)
        for r in range(N):
            i = np.argsort(o[r], axis=1)
            now[r] = ((now[r].astype(np.float32) + gcols(back, i).astype(np.float32)) * np.float32(0.5)).astype(BF)
    y, ol = np.zeros((N, 128, C), np.float32), np.zeros((N, 8, C), np.float32)
    oc, osc = np.zeros((N, 128, 4 * C), np.uint8), np.zeros((N, 16, C), np.uint8)
    for r in range(N):
        q = mx_ref.quantize(now[r])
        y[r] = mx_ref.matmul(mx_ref.quantize(v[r]), q)
        ol[r] = o[r]
        oc[r], osc[r] = emit(q)
    return {"y": y, "ol": ol, "oc": oc, "osc": osc}

@@ -1,0 +1,431 @@
+from concourse.bass import DstId, RemoteDMATransfer
+from concourse.mybir import dt, AluOpType, ActivationFunctionType
+
+A = AluOpType
+F = ActivationFunctionType
+C, R, N = 384, 3, 4
+Q = C // N
+K = C // 16
+H2 = C // 2
+PAD = 128 - Q
+NV = 13
+MID = 16
+GV = 8
+BV = 16
+LOW = 2.0 ** 90
+X4, U8, U16, I32, BF, FP = "float8_e4m3fn_x4", "uint8", "uint16", "int32", "bfloat16", "float32"
+
+_SB = dict(
+    xs=(4 * C, BF), us=(512, BF), vs=(512, BF), qx=(C, X4), qxs=(C, U8), qu=(128, X4), qus=(128, U8),
+    qb=(128, X4), qbs=(128, U8), qv=(128, X4), qvs=(128, U8), qw=(512, X4), qws=(512, U8),
+    ones=(512, BF), es=(2048, BF), qe=(512, X4), qes=(512, U8),
+    pi=(8, I32), pj=(8, I32), pf=(8, FP), uli=(8, I32), ul=(8, U16),
+    t16=(C, FP), t4=(C, BF), jr=(C, BF), jv=(C, BF), cap=(C, FP), rad=(C, FP), keep=(C, BF),
+    cap4=(C, BF), rad4=(C, BF), base=(K, FP), am=(C, FP), zz=(C, FP), eq=(C, BF), cr=(C, BF),
+    ck=(K, FP), fl=(K * C, BF), rs=(NV * H2, BF), gg=(K, FP), ll=(K, FP), lk=(K, FP), rk=(K, FP),
+    iw=(K, U16), iu=(K, U16), tm=(7 * K, FP), ow=(C, BF), a4=(C, BF), z4=(C, BF), off=(Q, U16), olf=(C, FP),
+    ss=(4 * (C + 2 * PAD), BF), qs=(512, X4), qss=(512, U8), ls=(3 * Q + PAD, X4), lss=(3 * Q + PAD, U8),
+    ms=(512, BF), qm=(128, X4), qms=(128, U8), hs=(512, BF), qh=(128, X4), qhs=(128, U8),
+    lh=(3 * Q, X4), lhs=(3 * Q, U8), sp=(4 * C, FP), ys=(C, FP))
+SCRATCH = {n: ("sbuf", [128, w], d) for n, (w, d) in _SB.items()}
+SCRATCH["ps"] = ("psum", [128, 8 * 512], FP)
+SEMAPHORES = (["sv", "sa", "sp", "sg", "ldx", "ldu", "ldw", "ldp", "sto", "stf"]
+              + ["%s%d" % (n, t) for n in ("aS", "lS", "lH") for t in range(R)]
+              + ["aH%d_%d" % (t, r) for t in range(R) for r in range(N)])
+
+
+def _near(topo, a, b):
+    ca, cb = topo.chip(a), topo.chip(b)
+    return 2 if topo.mates(ca, cb) else 1 if topo.same_plane(ca, cb) else 0
+
+
+def _bits(engines):
+    return sum(1 << e for e in engines)
+
+
+def rank_program(g, core, T, topo):
+    me = T.rank_of(core)
+    if me is None:
+        return
+    cores = list(T.cores)
+
+    def others(r):
+        return [d for d in range(N) if d != r]
+
+    def dests(r):
+        return sorted(others(r), key=lambda d: (_near(topo, cores[r], cores[d]), d))
+
+    def dst_id(d):
+        rid, pid, _ = topo.addr(cores[d])
+        return DstId(rid=rid, pnc=pid)
+
+    def halves(r, d):
+        e = topo.engines(cores[r], cores[d])
+        return e[:len(e) // 2], e[len(e) // 2:]
+
+    def wide(r):
+        e = [set(topo.engines(cores[r], cores[d])) for d in others(r)]
+        return sorted(e[0] & e[1] & e[2])
+
+    eng = {"v": g.vector, "a": g.scalar, "p": g.tensor, "g": g, "y": g.sync}
+    own = {"v": "sv", "a": "sa", "p": "sp", "g": "sg"}
+    known = {q: {} for q in eng}
+    count, writer, readers, group = {}, {}, {}, {}
+
+    def wait(q, toks):
+        for s, val, clock, _ in sorted(toks, key=lambda k: -k[1]):
+            if known[q].get(s, 0) < val:
+                eng[q].wait_ge(T.sem[s], val)
+                known[q][s] = val
+                for s2, v2 in clock.items():
+                    known[q][s2] = max(known[q].get(s2, 0), v2)
+
+    def before(q, r, w=(), x=()):
+        toks = [writer[k] for k in list(r) + list(x) if k in writer]
+        for k in w:
+            toks += readers.get(k, [])
+            if k in writer and not (q == "p" and writer[k][3] == "p"):
+                toks.append(writer[k])
+        for k in x:
+            toks += [t for t in readers.get(k, []) if t[3] != q]
+        wait(q, toks)
+
+    def after(tok, r, w):
+        for k in r:
+            readers.setdefault(k, []).append(tok)
+        for k in w:
+            writer[k] = tok
+            readers[k] = []
+
+    def op(q, name, args, r=(), w=(), x=(), **kw):
+        before(q, r, w, x)
+        e = eng[q]
+        call = {"copy": lambda: e.tensor_copy(*args), "tt": lambda: e.tensor_tensor(*args),
+                "ts": lambda: e.tensor_scalar(*args), "scan": lambda: e.tensor_tensor_scan(*args),
+                "set": lambda: e.memset(*args), "quant": lambda: e.quantize_mx(*args),
+                "act": lambda: e.activation(*args, **kw), "mm": lambda: e.matmul_mx(*args),
+                "iota": lambda: e.iota(*args, **kw), "sel": lambda: e.affine_select(*args)}[name]
+        s = own[q]
+        call().then_inc(T.sem[s], 1)
+        count[s] = count.get(s, 0) + 1
+        after([s, count[s], dict(known[q]), q], list(r) + list(x), w)
+
+    def shared(s, q, n, r, w=()):
+        count[s] = count.get(s, 0) + n
+        tok = group.setdefault(s, [s, 0, {}, "dma"])
+        tok[1] = count[s]
+        for s2, v2 in known[q].items():
+            tok[2][s2] = max(tok[2].get(s2, 0), v2)
+        after(tok, r, w)
+
+    def dma(q, out, in_, s, r=(), w=()):
+        before(q, r, w)
+        eng[q].dma_start(out, in_).then_inc(T.sem[s], 16)
+        shared(s, q, 16, r, w)
+
+    def send(d, out, in_, far, near, key):
+        rid, pid, _ = topo.addr(cores[d])
+        before("g", [key])
+        g.remote_dma(out, in_, T.sem[far], T.sem[near], pid, rid, topo.mask(core, cores[d]))
+        shared(near, "g", len(topo.engines(core, cores[d])), [key])
+
+    def arrive(s, n, w):
+        count[s] = n
+        after([s, n, {}, "far"], [], w)
+
+    def bank(b, n, a=0):
+        return T.ps[:, 512 * b + a:512 * b + a + n]
+
+    def u8(v):
+        return v.bitcast(dt.uint8)
+
+    XK = ["x0", "x1", "x2", "x3", "x4"]
+    MK = ["m0", "m1", "m2", "m3"]
+    flag = dict(allow_small_or_imprecise_dtypes=True)
+
+    dma("a", T.us[:], T.u[:], "ldu", w=["us"])
+    dma("y", T.xs[:, 0:2 * C], T.x[:, 0:2 * C], "ldx", w=XK[:2])
+    dma("a", T.xs[:, 2 * C:4 * C], T.x[:, 2 * C:4 * C], "ldx", w=XK[2:])
+
+    op("g", "iota", (T.t16[:], [[0, K], [1, 16]], 0, 0), w=["t16"], **flag)
+    op("g", "iota", (T.pi[:, 0:1], [[0, 1]], 0, 1), w=["pi"])
+    op("g", "iota", (T.uli[:], [[16, 8]], 0, 0), w=["uli"])
+    op("g", "iota", (T.t4[:], [[0, Q], [1, 4]], 0, 0), w=["t4"], **flag)
+    op("g", "iota", (T.jr[:], [[1, C]], -H2, 0), w=["jr"], **flag)
+    op("g", "iota", (T.base[:], [[16, K]], 16, 0), w=["base"], **flag)
+    op("v", "set", (T.ms[:], 0.0), w=MK)
+    op("v", "set", (T.hs[:, 4 * Q:512], 0.0), w=["hpad"])
+    op("v", "set", (T.ones[:], 1.0), w=["ones"])
+    op("v", "set", (T.ss[:, 0:4 * PAD], 0.0), w=["spad0"])
+    op("v", "set", (T.ss[:, 4 * (PAD + C):4 * (2 * PAD + C)], 0.0), w=["spad1"])
+    op("v", "set", (T.gg[:, K - 1:K], 0.0), w=["g%d" % (K - 1)])
+    op("v", "quant", (T.qm[:], T.qms[:], T.ms[:]), r=MK, w=["qm"])
+    op("v", "ts", (T.pj[:, 0:1], T.pi[:, 0:1], 15, None, A.bitwise_and), r=["pi"], w=["pj0"])
+    op("v", "ts", (T.pj[:, 1:2], T.pi[:, 0:1], 2, 3, A.logical_shift_right, A.bitwise_and), r=["pi"], w=["pj1"])
+    op("v", "ts", (T.pj[:, 2:3], T.pi[:, 0:1], 3, None, A.bitwise_and), r=["pi"], w=["pj2"])
+    op("v", "copy", (T.ul[:], T.uli[:]), r=["uli"], w=["ul"])
+    op("v", "copy", (T.pf[:, 0:3], T.pj[:, 0:3]), r=["pj0", "pj1", "pj2"], w=["pf"])
+    op("v", "ts", (T.cap[:], T.t16[:], T.pf[:, 0:1], -LOW, A.not_equal, A.mult), r=["t16", "pf"], w=["cap"])
+    op("v", "ts", (T.pf[:, 3:4], T.pf[:, 2:3], float(2 * C), None, A.add), r=["pf"], w=["pf3"])
+    op("a", "act", (T.keep[:], T.t16[:], F.Sign), r=["t16"], w=["keep"])
+    op("a", "act", (T.rad[:], T.keep[:], F.Identity), r=["keep"], w=["rad"], scale=4 * LOW, bias=-4 * LOW)
+    op("v", "quant", (T.qu[:], T.qus[:], T.us[:]), r=["us"], w=["qu"])
+    op("v", "copy", (T.qb[:, 0:128].bitcast(dt.uint32), T.qu[:, 0:128].bitcast(dt.uint32).indirect(T.ul[:, 0:8])),
+       r=["qu", "ul"], w=["qb"])
+    op("a", "act", (T.qbs[:, 0:128], T.qus[:, 0:128].indirect(T.ul[:, 0:8]), F.Copy), r=["qu", "ul"], w=["qbs"])
+    op("a", "act", (T.jv[:], T.jr[:], F.Copy), r=["jr"], w=["jv"], scale=1.0 / 512)
+    for b in range(4):
+        op("g", "sel", (T.es[:, 512 * b:512 * b + 512], T.ones[:], [[1, 512]], A.is_equal, 0.0, -b, -4),
+           r=["ones"], w=["e%d" % b])
+    wait("y", [writer["x0"]])
+    dma("y", u8(T.qw[:]), T.wc[:], "ldw", w=["qw"])
+    dma("y", T.qws[:], T.ws[:], "ldw", w=["qw2"])
+    dma("y", T.vs[:], T.v[:], "ldw", w=["vs"])
+    dma("y", u8(T.ls[:, 3 * Q:3 * Q + PAD]), u8(T.qm[:, 0:PAD]), "ldp", r=["qm"], w=["lpad"])
+    dma("y", T.lss[:, 3 * Q:3 * Q + PAD], T.qms[:, 0:PAD], "ldp", r=["qm"], w=["lpad2"])
+
+    order = dests(me) + [me]
+    shift = [Q * (order.index(q) - q) for q in range(N)]
+    cut = 16 * NV
+
+    for t in range(R):
+        op("v", "quant", (T.qx[:], T.qxs[:], T.xs[:]), r=XK, w=["qx"])
+        for b in range(2):
+            op("p", "mm", (bank(b, C), T.qb[:], T.qbs[:], T.qx[:], T.qxs[:], True, True),
+               r=["qb", "qbs", "qx"], w=["b%d" % b])
+        if t == 0:
+            op("v", "ts", (T.cap4[:], T.t4[:], T.pf[:, 1:2], 0.5, A.is_equal, A.subtract), r=["t4", "pf"], w=["cap4"])
+        for n, (a, z) in enumerate(((cut, C), (0, cut))):
+            op("v", "tt", (T.am[:, a:z], bank(0, z - a, a), T.cap[:, a:z], A.add), r=["cap"], w=["am%d" % n], x=["b0"])
+            if n == 1:
+                op("v", "scan", (T.zz[:, a:z], T.rad[:, a:z], T.am[:, a:z], 0.0, A.add, A.max), r=["rad", "am1"], w=["z1"])
+            else:
+                op("v", "scan", (T.zz[:, a:z], T.rad[:, a:z], T.am[:, a:z], 0.0, A.add, A.max), r=["rad", "am0"], w=["z0"])
+
+        def sign(c):
+            op("a", "act", (T.fl[:, C * c:C * c + C], bank(1, C), F.Sign), r=["z0"], w=["f%d" % c, "h%d" % c], x=["b1"],
+               bias=T.zz[:, 16 * c + 15:16 * c + 16], scale=-1.0)
+
+        def tally(c):
+            m = C * c + 16 * c + 16
+            op("a", "act", (T.fl[:, C * c:m], T.fl[:, C * c:m], F.Relu), r=["f%d" % c], w=["f%d" % c, "l%d" % c],
+               accum_out=T.ll[:, c:c + 1])
+            if c < K - 1:
+                op("a", "act", (T.fl[:, m:C * c + C], T.fl[:, m:C * c + C], F.Relu), r=["h%d" % c],
+                   w=["h%d" % c, "g%d" % c], scale=-1.0, accum_out=T.gg[:, c:c + 1])
+
+        sign(K - 1)
+        for c in range(K - 1, NV - 1, -1):
+            if c > NV:
+                sign(c - 1)
+            tally(c)
+
+        def compare(c):
+            m = 16 * c + 16
+            s = T.zz[:, m - 1:m]
+            op("v", "ts", (T.fl[:, C * c:C * c + m], bank(0, m), s, 0.5, A.is_ge, A.subtract),
+               r=["z1"], w=["f%d" % c], x=["b0"])
+            op("v", "ts", (T.fl[:, C * c + m:C * c + C], bank(0, C - m, m), s, 0.5, A.is_gt, A.subtract),
+               r=["z1"], w=["h%d" % c], x=["b0"])
+
+        def place(a, z, key):
+            op("v", "copy", (T.ow[:, 0:C].indirect(T.iw[:, a:z]), T.jv[:, 16 * a:16 * z]), r=[key, "jv"], w=["ow"])
+
+        def lower(a, z):
+            op("v", "tt", (T.lk[:, a:z], T.ck[:, a:z], T.ll[:, a:z], A.subtract),
+               r=["ck"] + ["l%d" % k for k in range(a, z)], w=["lk%d" % a])
+
+        def upper(a, z):
+            op("v", "tt", (T.rk[:, a:z], T.gg[:, a:z], T.lk[:, a:z], A.add),
+               r=["lk%d" % a] + ["g%d" % k for k in range(a, z)], w=["rk%d" % a])
+
+        def narrow(a, z):
+            op("v", "copy", (T.iw[:, a:z], T.rk[:, a:z]), r=["rk%d" % a], w=["iw%d" % a])
+
+        op("v", "tt", (T.eq[:], bank(0, C), T.zz[:], A.is_equal), r=["z0", "z1"], w=["eq"], x=["b0"])
+        compare(0)
+        op("v", "scan", (T.cr[:], T.keep[:], T.eq[:], 0.0, A.mult, A.subtract), r=["keep", "eq"], w=["cr"])
+        for c in range(NV):
+            if c + 1 < NV:
+                compare(c + 1)
+            if c == 0:
+                op("v", "tt", (T.ck[:], T.cr[:, 15:C:16], T.base[:], A.add), r=["cr", "base"], w=["ck"])
+                if t == 0:
+                    op("v", "ts", (T.rad4[:], T.t4[:], 0.5, -2.0, A.is_lt, A.mult), r=["t4"], w=["rad4"])
+            if c == NV - 1:
+                lower(MID, K)
+            op("v", "scan", (T.rs[:, H2 * c:H2 * c + H2], T.fl[:, C * c:C * c + H2], T.fl[:, C * c + H2:C * c + C],
+                             T.cr[:, 16 * c + 15:16 * c + 16], A.add, A.add), r=["f%d" % c, "h%d" % c, "cr"], w=["r%d" % c])
+        even = NV - NV % 2
+        IK = ["iw0", "iw%d" % NV, "iw%d" % MID]
+        upper(MID, K)
+        op("v", "ts", (T.iw[:, 0:NV], T.rs[:, H2 - 1:H2 * NV:H2], float(H2), None, A.add),
+           r=["r%d" % k for k in range(NV)], w=["iw0"])
+        narrow(MID, K)
+        place(0, even, IK[0])
+        place(MID, K, IK[2])
+        lower(NV, MID)
+        upper(NV, MID)
+        narrow(NV, MID)
+        place(even, MID, IK[1])
+
+        op("v", "scan", (T.a4[:], T.ow[:], T.cap4[:], -1.0, A.max, A.min), r=["ow", "cap4"], w=["a4"])
+        op("v", "scan", (T.z4[:], T.rad4[:], T.a4[:], 0.0, A.add, A.max), r=["rad4", "a4"], w=["z4"])
+        op("v", "ts", (T.off[:], T.z4[:, 3:C:4], 2048.0, T.pf[:, 3:4], A.mult, A.add), r=["z4", "pf3"], w=["off"])
+
+        def gather(q, k):
+            o, s = K * order[k], 4 * (PAD + Q * k)
+            if q == "v":
+                op("v", "copy", (T.ss[:, s:s + 16 * GV], T.xs[:, 0:4 * C].indirect(T.off[:, o:o + GV])),
+                   r=XK + ["off"], w=["sv%d" % k])
+            else:
+                op("a", "act", (T.ss[:, s + 16 * GV:s + 4 * Q], T.xs[:, 0:4 * C].indirect(T.off[:, o + GV:o + K]), F.Copy),
+                   r=XK + ["off"], w=["sa%d" % k])
+
+        def pack(k):
+            s = 4 * Q * k + (4 * PAD if k == 3 else 0)
+            edge = "spad0" if k == 0 else "spad1" if k == 3 else "sa%d" % (k - 1)
+            op("v", "quant", (T.qs[:, 128 * k:128 * k + 128], T.qss[:, 128 * k:128 * k + 128], T.ss[:, s:s + 512]),
+               r=["sv%d" % k, "sa%d" % k, edge], w=["qs%d" % k])
+
+        lS, aS, lH = "lS%d" % t, "aS%d" % t, "lH%d" % t
+
+        def ends(k, codes):
+            s, l = 128 * k + PAD, Q * others(order[k]).index(me)
+            if codes:
+                return u8(T.ls[:, l:l + Q]), u8(T.qs[:, s:s + Q])
+            return T.lss[:, l:l + Q], T.qss[:, s:s + Q]
+
+        def write_pair():
+            tr = []
+            for k in range(2):
+                out, in_ = ends(k, False)
+                e = halves(me, order[k])[k]
+                tr.append(RemoteDMATransfer(dst_ids=[dst_id(order[k])], dma_engine_mask=_bits(e), remote_sem=T.sem[aS],
+                                            srcs=[in_], dsts=[out]))
+                shared(lS, "g", len(e), ["qs%d" % k])
+            g.remote_dma_fused(tr, local_sem=T.sem[lS])
+
+        for k in range(4):
+            gather("a", k)
+        gather("v", 0)
+        for k in range(3):
+            gather("v", k + 1)
+            pack(k)
+            send(order[k], *ends(k, True), aS, lS, "qs%d" % k)
+            if k == 1:
+                write_pair()
+            if k == 2:
+                send(order[k], *ends(k, False), aS, lS, "qs%d" % k)
+        pack(3)
+        total = 0
+        for r in others(me):
+            k, full = dests(r).index(me), len(topo.engines(cores[r], core))
+            total += full + (full if k == 2 else len(halves(r, me)[k]))
+        arrive(aS, total, ["ls"])
+
+        if t == 0:
+            op("v", "quant", (T.qe[:], T.qes[:], T.es[:]), r=["e0", "e1", "e2", "e3"], w=["qe"])
+            op("v", "quant", (T.qv[:], T.qvs[:], T.vs[:]), r=["vs"], w=["qv"])
+        tm = [T.tm[:, K * i:K * i + K] for i in range(7)]
+        for q in range(1, N):
+            op("v", "ts", (tm[q - 1], T.iw[:], float(Q * q), float(shift[q] - shift[q - 1]), A.is_ge, A.mult),
+               r=IK, w=["tm%d" % (q - 1)])
+        op("v", "ts", (tm[3], T.iw[:], float(shift[0]), None, A.add), r=IK, w=["tm3"])
+        op("v", "tt", (tm[4], tm[0], tm[1], A.add), r=["tm0", "tm1"], w=["tm4"])
+        op("v", "tt", (tm[5], tm[2], tm[3], A.add), r=["tm2", "tm3"], w=["tm5"])
+        op("v", "tt", (tm[6], tm[4], tm[5], A.add), r=["tm4", "tm5"], w=["tm6"])
+        op("v", "copy", (T.iu[:], tm[6]), r=["tm6"], w=["iu"])
+        if t == R - 1:
+            op("v", "ts", (T.olf[:], T.ow[:], 512.0, float(H2), A.mult, A.add), r=["ow"], w=["olf"])
+            dma("y", T.ol[:], T.olf[0:128:16, :], "sto", r=["olf"])
+
+        def unpack(bk, b, n, codes, scales, keys, start=True, stop=True):
+            op("p", "mm", (bank(bk, n), T.qe[:, 128 * b:128 * b + 128], T.qes[:, 128 * b:128 * b + 128], codes, scales,
+                           start, stop), r=["qe"] + keys, w=["b%d" % bk])
+
+        def term(b, r, start, stop):
+            if r == me:
+                unpack(b, b, 128, T.qs[:, 384:512], T.qss[:, 384:512], ["qs3"], start, stop)
+            else:
+                l = Q * others(me).index(r)
+                unpack(b, b, 128, T.ls[:, l:l + 128], T.lss[:, l:l + 128], ["ls", "lpad", "lpad2"], start, stop)
+
+        seq = [1, 0, 2, 3] if me == 1 else list(range(N))
+        early = 1 if seq[0] == me else 0
+        for b in range(4 * early):
+            term(b, me, True, False)
+        for b in range(4):
+            for i in range(early, N):
+                term(b, seq[i], i == 0, i == N - 1)
+            if b % 2 == 0:
+                op("a", "act", (T.ms[:, b:4 * Q:4], bank(b, Q), F.Copy), w=[MK[b]], x=["b%d" % b], scale=0.25)
+            else:
+                op("v", "ts", (T.ms[:, b:4 * Q:4], bank(b, Q), 0.25, None, A.mult), w=[MK[b]], x=["b%d" % b])
+        op("v", "quant", (T.qm[:], T.qms[:], T.ms[:]), r=MK, w=["qm"])
+
+        for b in range(4):
+            op("p", "mm", (bank(4 + b, 128), T.qw[:, 128 * b:128 * b + 128], T.qws[:, 128 * b:128 * b + 128],
+                           T.qm[:], T.qms[:], True, True), r=["qw", "qw2", "qm"], w=["b%d" % (4 + b)])
+            if b % 2 == 0:
+                op("a", "act", (T.hs[:, b:4 * Q:4], bank(4 + b, Q), F.Relu), w=["hs%d" % b], x=["b%d" % (4 + b)], scale=0.0625)
+            else:
+                op("v", "ts", (T.hs[:, b:4 * Q:4], bank(4 + b, Q), 0.0, 0.0625, A.max, A.mult),
+                   w=["hs%d" % b], x=["b%d" % (4 + b)])
+        op("v", "quant", (T.qh[:], T.qhs[:], T.hs[:]), r=["hs0", "hs1", "hs2", "hs3", "hpad"], w=["qh"])
+
+        before("g", ["qh"])
+        e = wide(me)
+        at = [Q * ((dests(d).index(me) + 1) % 3) for d in order[:3]]
+        aH = "aH%d_%d" % (t, me)
+        g.remote_dma_fused([RemoteDMATransfer(dst_ids=[dst_id(d) for d in order[:3]], dma_engine_mask=_bits(e),
+                                              remote_sem=T.sem[aH], srcs=[T.qhs[:, 0:Q]],
+                                              dsts=[T.lhs[:, l:l + Q] for l in at])], local_sem=T.sem[lH])
+        shared(lH, "g", len(e), ["qh"])
+        for d, l in zip(order[:3], at):
+            send(d, u8(T.lh[:, l:l + Q]), u8(T.qh[:, 0:Q]), aH, lH, "qh")
+        for k, r in enumerate(order[:3]):
+            arrive("aH%d_%d" % (t, r), len(wide(r)) + len(topo.engines(cores[r], core)), ["lh%d" % k])
+
+        def add(bk, b, k, n, key):
+            s = 4 * (PAD + Q * k) + b
+            op("v", "tt", (T.sp[:, C * b + Q * k:C * b + Q * (k + n)], bank(bk, Q * n), T.ss[:, s:s + 4 * Q * n:4], A.add),
+               r=["s%s%d" % (q, i) for q in "va" for i in range(k, k + n)], w=[key], x=["b%d" % bk])
+
+        def back(q, b, a, z, key):
+            win = T.sp[:, C * b:C * b + C].indirect(T.iu[:, a:z])
+            out, keys = T.xs[:, 64 * a + b:64 * z:4], ["po%d" % b, "pa%d" % b, "pb%d" % b, "iu"]
+            if q == "a":
+                op("a", "act", (out, win, F.Copy), r=keys, w=[key], scale=0.5)
+            else:
+                op("v", "ts", (out, win, 0.5, None, A.mult), r=keys, w=[key])
+
+        for b in range(4):
+            unpack(b, b, 128, T.qh[:], T.qhs[:], ["qh"])
+            add(b, b, 3, 1, "po%d" % b)
+        for b in range(4):
+            unpack(4 + b, b, 2 * Q, T.lh[:, Q:3 * Q], T.lhs[:, Q:3 * Q], ["lh0", "lh1"])
+            add(4 + b, b, 0, 2, "pa%d" % b)
+        for b in range(4):
+            unpack(b, b, 128, T.lh[:, 0:128], T.lhs[:, 0:128], ["lh2"])
+        for b in range(4):
+            add(b, b, 2, 1, "pb%d" % b)
+            if b < 2:
+                back("a", b, 0, K, XK[b])
+        back("v", 2, 0, K, XK[2])
+        back("a", 3, BV, K, XK[4])
+        back("v", 3, 0, BV, XK[3])
+
+    op("v", "quant", (T.qx[:], T.qxs[:], T.xs[:]), r=XK, w=["qx"])
+    for h in range(2):
+        op("p", "mm", (bank(h, H2), T.qv[:], T.qvs[:], T.qx[:, H2 * h:H2 * h + H2], T.qxs[:, H2 * h:H2 * h + H2], True, True),
+           r=["qv", "qx"], w=["b%d" % h])
+    dma("y", T.oc[:], u8(T.qx[:]), "stf", r=["qx"])
+    op("v", "copy", (T.ys[:, 0:H2], bank(0, H2)), w=["y0"], x=["b0"])
+    for k in range(4):
+        dma("a" if k == 0 else "y", T.osc[4 * k:4 * k + 4, :], T.qxs[32 * k:32 * k + 4, :], "stf", r=["qx"])
+    op("a", "act", (T.ys[:, H2:C], bank(1, H2), F.Copy), w=["y1"], x=["b1"])
+    dma("a", T.y[:], T.ys[:], "stf", r=["y0", "y1"])
+    for s in SEMAPHORES:
+        if count.get(s, 0) > known["g"].get(s, 0):
+            g.wait_ge(T.sem[s], count[s])

@@ -10,8 +10,8 @@ H2 = C // 2
 PAD = 128 - Q
 NV = 13
 MID = 16
-GV = 8
-BV = 16
+GV = (12, 4, 8, 10)
+BV = 20
 LOW = 2.0 ** 90
 X4, U8, U16, I32, BF, FP = "float8_e4m3fn_x4", "uint8", "uint16", "int32", "bfloat16", "float32"
 
@@ -24,14 +24,14 @@ _SB = dict(
     cap4=(C, BF), rad4=(C, BF), base=(K, FP), am=(C, FP), zz=(C, FP), eq=(C, BF), cr=(C, BF),
     ck=(K, FP), fl=(K * C, BF), rs=(NV * H2, BF), gg=(K, FP), ll=(K, FP), lk=(K, FP), rk=(K, FP),
     iw=(K, U16), iu=(K, U16), tm=(7 * K, FP), ow=(C, BF), a4=(C, BF), z4=(C, BF), off=(Q, U16), olf=(C, FP),
-    ss=(4 * (C + 2 * PAD), BF), qs=(512, X4), qss=(512, U8), ls=(3 * Q + PAD, X4), lss=(3 * Q + PAD, U8),
+    ss=(4 * (C + 2 * PAD), BF), qs=(512, X4), qss=(512, U8), ls=(3 * 128, X4), lss=(3 * 128, U8),
     ms=(512, BF), qm=(128, X4), qms=(128, U8), hs=(512, BF), qh=(128, X4), qhs=(128, U8),
-    lh=(3 * Q, X4), lhs=(3 * Q, U8), sp=(4 * C, FP), ys=(C, FP))
+    lh=(3 * Q + PAD, X4), lhs=(3 * Q + PAD, U8), sp=(4 * C, FP), ys=(C, FP))
 SCRATCH = {n: ("sbuf", [128, w], d) for n, (w, d) in _SB.items()}
 SCRATCH["ps"] = ("psum", [128, 8 * 512], FP)
 SEMAPHORES = (["sv", "sa", "sp", "sg", "ldx", "ldu", "ldw", "ldp", "sto", "stf"]
-              + ["%s%d" % (n, t) for n in ("aS", "lS", "lH") for t in range(R)]
-              + ["aH%d_%d" % (t, r) for t in range(R) for r in range(N)])
+              + ["%s%d" % (n, t) for n in ("lS", "lH") for t in range(R)]
+              + ["%s%d_%d" % (n, t, r) for n in ("aS", "aH") for t in range(R) for r in range(N)])
 
 
 def _near(topo, a, b):
@@ -66,6 +66,12 @@ def rank_program(g, core, T, topo):
     def wide(r):
         e = [set(topo.engines(cores[r], cores[d])) for d in others(r)]
         return sorted(e[0] & e[1] & e[2])
+
+    def slot_s(r, d):
+        return 128 * others(d).index(r)
+
+    def slot_h(r, d):
+        return Q * (2 - dests(d).index(r))
 
     eng = {"v": g.vector, "a": g.scalar, "p": g.tensor, "g": g, "y": g.sync}
     own = {"v": "sv", "a": "sa", "p": "sp", "g": "sg"}
@@ -173,6 +179,7 @@ def rank_program(g, core, T, topo):
     op("v", "copy", (T.qb[:, 0:128].bitcast(dt.uint32), T.qu[:, 0:128].bitcast(dt.uint32).indirect(T.ul[:, 0:8])),
        r=["qu", "ul"], w=["qb"])
     op("a", "act", (T.qbs[:, 0:128], T.qus[:, 0:128].indirect(T.ul[:, 0:8]), F.Copy), r=["qu", "ul"], w=["qbs"])
+    op("v", "ts", (T.cap4[:], T.t4[:], T.pf[:, 1:2], 0.5, A.is_equal, A.subtract), r=["t4", "pf"], w=["cap4"])
     op("a", "act", (T.jv[:], T.jr[:], F.Copy), r=["jr"], w=["jv"], scale=1.0 / 512)
     for b in range(4):
         op("g", "sel", (T.es[:, 512 * b:512 * b + 512], T.ones[:], [[1, 512]], A.is_equal, 0.0, -b, -4),
@@ -181,30 +188,38 @@ def rank_program(g, core, T, topo):
     dma("y", u8(T.qw[:]), T.wc[:], "ldw", w=["qw"])
     dma("y", T.qws[:], T.ws[:], "ldw", w=["qw2"])
     dma("y", T.vs[:], T.v[:], "ldw", w=["vs"])
-    dma("y", u8(T.ls[:, 3 * Q:3 * Q + PAD]), u8(T.qm[:, 0:PAD]), "ldp", r=["qm"], w=["lpad"])
-    dma("y", T.lss[:, 3 * Q:3 * Q + PAD], T.qms[:, 0:PAD], "ldp", r=["qm"], w=["lpad2"])
+    for i in range(3):
+        dma("y", u8(T.ls[:, 128 * i + Q:128 * i + 128]), u8(T.qm[:, 0:PAD]), "ldp", r=["qm"], w=["lpad%d" % i])
+        dma("y", T.lss[:, 128 * i + Q:128 * i + 128], T.qms[:, 0:PAD], "ldp", r=["qm"], w=["lspad%d" % i])
+    dma("y", u8(T.lh[:, 3 * Q:3 * Q + PAD]), u8(T.qm[:, 0:PAD]), "ldp", r=["qm"], w=["hp0"])
+    dma("y", T.lhs[:, 3 * Q:3 * Q + PAD], T.qms[:, 0:PAD], "ldp", r=["qm"], w=["hp1"])
 
     order = dests(me) + [me]
     shift = [Q * (order.index(q) - q) for q in range(N)]
-    cut = 16 * NV
+    top = C - 128
+    QK = ["qx0", "qx1"]
 
     for t in range(R):
-        op("v", "quant", (T.qx[:], T.qxs[:], T.xs[:]), r=XK, w=["qx"])
+        op("v", "quant", (T.qx[:, top:C], T.qxs[:, top:C], T.xs[:, 4 * top:4 * C]), r=XK, w=["qx0"])
+        op("p", "mm", (bank(2, C - top), T.qb[:], T.qbs[:], T.qx[:, top:C], T.qxs[:, top:C], True, True),
+           r=["qb", "qbs", "qx0"], w=["b2"])
+        op("v", "quant", (T.qx[:, 0:top], T.qxs[:, 0:top], T.xs[:, 0:4 * top]), r=XK, w=["qx1"])
         for b in range(2):
             op("p", "mm", (bank(b, C), T.qb[:], T.qbs[:], T.qx[:], T.qxs[:], True, True),
-               r=["qb", "qbs", "qx"], w=["b%d" % b])
-        if t == 0:
-            op("v", "ts", (T.cap4[:], T.t4[:], T.pf[:, 1:2], 0.5, A.is_equal, A.subtract), r=["t4", "pf"], w=["cap4"])
-        for n, (a, z) in enumerate(((cut, C), (0, cut))):
-            op("v", "tt", (T.am[:, a:z], bank(0, z - a, a), T.cap[:, a:z], A.add), r=["cap"], w=["am%d" % n], x=["b0"])
-            if n == 1:
-                op("v", "scan", (T.zz[:, a:z], T.rad[:, a:z], T.am[:, a:z], 0.0, A.add, A.max), r=["rad", "am1"], w=["z1"])
-            else:
-                op("v", "scan", (T.zz[:, a:z], T.rad[:, a:z], T.am[:, a:z], 0.0, A.add, A.max), r=["rad", "am0"], w=["z0"])
+               r=["qb", "qbs"] + QK, w=["b%d" % b])
+        span = {0: (top, C, 2), 1: (0, top, 0)}
+        for n in range(2):
+            a, z, bk = span[n]
+            op("v", "tt", (T.am[:, a:z], bank(bk, z - a), T.cap[:, a:z], A.add), r=["cap"], w=["am%d" % n],
+               x=["b%d" % bk])
+            if t == 0 and n == 0:
+                op("v", "ts", (T.rad4[:], T.t4[:], 0.5, -2.0, A.is_lt, A.mult), r=["t4"], w=["rad4"])
+            op("v", "scan", (T.zz[:, a:z], T.rad[:, a:z], T.am[:, a:z], 0.0, A.add, A.max),
+               r=["rad", "am%d" % n], w=["z%d" % n])
 
         def sign(c):
-            op("a", "act", (T.fl[:, C * c:C * c + C], bank(1, C), F.Sign), r=["z0"], w=["f%d" % c, "h%d" % c], x=["b1"],
-               bias=T.zz[:, 16 * c + 15:16 * c + 16], scale=-1.0)
+            op("a", "act", (T.fl[:, C * c:C * c + C], bank(1, C), F.Sign), r=["z0" if 16 * c >= top else "z1"],
+               w=["f%d" % c, "h%d" % c], x=["b1"], bias=T.zz[:, 16 * c + 15:16 * c + 16], scale=-1.0)
 
         def tally(c):
             m = C * c + 16 * c + 16
@@ -228,8 +243,8 @@ def rank_program(g, core, T, topo):
             op("v", "ts", (T.fl[:, C * c + m:C * c + C], bank(0, C - m, m), s, 0.5, A.is_gt, A.subtract),
                r=["z1"], w=["h%d" % c], x=["b0"])
 
-        def place(a, z, key):
-            op("v", "copy", (T.ow[:, 0:C].indirect(T.iw[:, a:z]), T.jv[:, 16 * a:16 * z]), r=[key, "jv"], w=["ow"])
+        def place(a, z, keys):
+            op("v", "copy", (T.ow[:, 0:C].indirect(T.iw[:, a:z]), T.jv[:, 16 * a:16 * z]), r=keys + ["jv"], w=["ow"])
 
         def lower(a, z):
             op("v", "tt", (T.lk[:, a:z], T.ck[:, a:z], T.ll[:, a:z], A.subtract),
@@ -242,6 +257,10 @@ def rank_program(g, core, T, topo):
         def narrow(a, z):
             op("v", "copy", (T.iw[:, a:z], T.rk[:, a:z]), r=["rk%d" % a], w=["iw%d" % a])
 
+        def single(c):
+            op("v", "ts", (T.iw[:, c:c + 1], T.gg[:, c:c + 1], T.ck[:, c:c + 1], T.ll[:, c:c + 1], A.add, A.subtract),
+               r=["ck", "g%d" % c, "l%d" % c], w=["iw%d" % c])
+
         op("v", "tt", (T.eq[:], bank(0, C), T.zz[:], A.is_equal), r=["z0", "z1"], w=["eq"], x=["b0"])
         compare(0)
         op("v", "scan", (T.cr[:], T.keep[:], T.eq[:], 0.0, A.mult, A.subtract), r=["keep", "eq"], w=["cr"])
@@ -250,37 +269,43 @@ def rank_program(g, core, T, topo):
                 compare(c + 1)
             if c == 0:
                 op("v", "tt", (T.ck[:], T.cr[:, 15:C:16], T.base[:], A.add), r=["cr", "base"], w=["ck"])
-                if t == 0:
-                    op("v", "ts", (T.rad4[:], T.t4[:], 0.5, -2.0, A.is_lt, A.mult), r=["t4"], w=["rad4"])
             if c == NV - 1:
                 lower(MID, K)
             op("v", "scan", (T.rs[:, H2 * c:H2 * c + H2], T.fl[:, C * c:C * c + H2], T.fl[:, C * c + H2:C * c + C],
                              T.cr[:, 16 * c + 15:16 * c + 16], A.add, A.add), r=["f%d" % c, "h%d" % c, "cr"], w=["r%d" % c])
         even = NV - NV % 2
-        IK = ["iw0", "iw%d" % NV, "iw%d" % MID]
+        IK = ["iw0", "iw%d" % MID] + ["iw%d" % c for c in range(NV, MID)]
         upper(MID, K)
         op("v", "ts", (T.iw[:, 0:NV], T.rs[:, H2 - 1:H2 * NV:H2], float(H2), None, A.add),
            r=["r%d" % k for k in range(NV)], w=["iw0"])
         narrow(MID, K)
-        place(0, even, IK[0])
-        place(MID, K, IK[2])
-        lower(NV, MID)
-        upper(NV, MID)
-        narrow(NV, MID)
-        place(even, MID, IK[1])
+        place(0, even, IK[:1])
+        single(MID - 1)
+        place(MID, K, IK[1:2])
+        for c in range(MID - 2, NV - 1, -1):
+            single(c)
+        place(even, MID, IK)
 
-        op("v", "scan", (T.a4[:], T.ow[:], T.cap4[:], -1.0, A.max, A.min), r=["ow", "cap4"], w=["a4"])
-        op("v", "scan", (T.z4[:], T.rad4[:], T.a4[:], 0.0, A.add, A.max), r=["rad4", "a4"], w=["z4"])
-        op("v", "ts", (T.off[:], T.z4[:, 3:C:4], 2048.0, T.pf[:, 3:4], A.mult, A.add), r=["z4", "pf3"], w=["off"])
+        def lay(step, qs):
+            a, z = Q * min(qs), Q * (max(qs) + 1)
+            ka, kz, ko = ["a4%d" % q for q in qs], ["z4%d" % q for q in qs], ["off%d" % q for q in qs]
+            if step == 0:
+                op("v", "scan", (T.a4[:, a:z], T.ow[:, a:z], T.cap4[:, a:z], -1.0, A.max, A.min), r=["ow", "cap4"], w=ka)
+            elif step == 1:
+                op("v", "scan", (T.z4[:, a:z], T.rad4[:, a:z], T.a4[:, a:z], 0.0, A.add, A.max), r=["rad4"] + ka, w=kz)
+            else:
+                op("v", "ts", (T.off[:, a // 4:z // 4], T.z4[:, a + 3:z:4], 2048.0, T.pf[:, 3:4], A.mult, A.add),
+                   r=kz + ["pf3"], w=ko)
 
         def gather(q, k):
-            o, s = K * order[k], 4 * (PAD + Q * k)
+            o, s, n = K * order[k], 4 * (PAD + Q * k), GV[k]
+            keys = XK + ["off%d" % order[k]]
             if q == "v":
-                op("v", "copy", (T.ss[:, s:s + 16 * GV], T.xs[:, 0:4 * C].indirect(T.off[:, o:o + GV])),
-                   r=XK + ["off"], w=["sv%d" % k])
+                op("v", "copy", (T.ss[:, s:s + 16 * n], T.xs[:, 0:4 * C].indirect(T.off[:, o:o + n])),
+                   r=keys, w=["sv%d" % k])
             else:
-                op("a", "act", (T.ss[:, s + 16 * GV:s + 4 * Q], T.xs[:, 0:4 * C].indirect(T.off[:, o + GV:o + K]), F.Copy),
-                   r=XK + ["off"], w=["sa%d" % k])
+                op("a", "act", (T.ss[:, s + 16 * n:s + 4 * Q], T.xs[:, 0:4 * C].indirect(T.off[:, o + n:o + K]), F.Copy),
+                   r=keys, w=["sa%d" % k])
 
         def pack(k):
             s = 4 * Q * k + (4 * PAD if k == 3 else 0)
@@ -288,10 +313,10 @@ def rank_program(g, core, T, topo):
             op("v", "quant", (T.qs[:, 128 * k:128 * k + 128], T.qss[:, 128 * k:128 * k + 128], T.ss[:, s:s + 512]),
                r=["sv%d" % k, "sa%d" % k, edge], w=["qs%d" % k])
 
-        lS, aS, lH = "lS%d" % t, "aS%d" % t, "lH%d" % t
+        lS, aS, lH = "lS%d" % t, "aS%d_%d" % (t, me), "lH%d" % t
 
         def ends(k, codes):
-            s, l = 128 * k + PAD, Q * others(order[k]).index(me)
+            s, l = 128 * k + PAD, slot_s(me, order[k])
             if codes:
                 return u8(T.ls[:, l:l + Q]), u8(T.qs[:, s:s + Q])
             return T.lss[:, l:l + Q], T.qss[:, s:s + Q]
@@ -306,23 +331,37 @@ def rank_program(g, core, T, topo):
                 shared(lS, "g", len(e), ["qs%d" % k])
             g.remote_dma_fused(tr, local_sem=T.sem[lS])
 
-        for k in range(4):
-            gather("a", k)
-        gather("v", 0)
-        for k in range(3):
-            gather("v", k + 1)
+        def leave(k):
             pack(k)
             send(order[k], *ends(k, True), aS, lS, "qs%d" % k)
-            if k == 1:
-                write_pair()
-            if k == 2:
-                send(order[k], *ends(k, False), aS, lS, "qs%d" % k)
+
+        runs = [order[0:2]] if abs(order[0] - order[1]) == 1 else [order[0:1], order[1:2]]
+        for qs in runs:
+            for step in range(3):
+                lay(step, qs)
+        gather("a", 0)
+        gather("a", 1)
+        gather("v", 0)
+        lay(0, order[2:3])
+        leave(0)
+        lay(1, order[2:3])
+        gather("v", 1)
+        lay(2, order[2:3])
+        gather("a", 2)
+        leave(1)
+        write_pair()
+        gather("v", 2)
+        lay(0, order[3:4])
+        leave(2)
+        send(order[2], *ends(2, False), aS, lS, "qs2")
+        lay(1, order[3:4])
+        lay(2, order[3:4])
+        gather("a", 3)
+        gather("v", 3)
         pack(3)
-        total = 0
         for r in others(me):
             k, full = dests(r).index(me), len(topo.engines(cores[r], core))
-            total += full + (full if k == 2 else len(halves(r, me)[k]))
-        arrive(aS, total, ["ls"])
+            arrive("aS%d_%d" % (t, r), full + (full if k == 2 else len(halves(r, me)[k])), ["ls%d" % r])
 
         if t == 0:
             op("v", "quant", (T.qe[:], T.qes[:], T.es[:]), r=["e0", "e1", "e2", "e3"], w=["qe"])
@@ -348,13 +387,15 @@ def rank_program(g, core, T, topo):
             if r == me:
                 unpack(b, b, 128, T.qs[:, 384:512], T.qss[:, 384:512], ["qs3"], start, stop)
             else:
-                l = Q * others(me).index(r)
-                unpack(b, b, 128, T.ls[:, l:l + 128], T.lss[:, l:l + 128], ["ls", "lpad", "lpad2"], start, stop)
+                l = slot_s(r, me)
+                unpack(b, b, 128, T.ls[:, l:l + 128], T.lss[:, l:l + 128],
+                       ["ls%d" % r, "lpad%d" % (l // 128), "lspad%d" % (l // 128)], start, stop)
 
-        seq = [1, 0, 2, 3] if me == 1 else list(range(N))
-        early = 1 if seq[0] == me else 0
-        for b in range(4 * early):
-            term(b, me, True, False)
+        seq = sorted(range(2), key=lambda r: -1 if r == me else dests(r).index(me)) + [2, 3]
+        early = seq.index(order[2])
+        for i in range(early):
+            for b in range(4):
+                term(b, seq[i], i == 0, False)
         for b in range(4):
             for i in range(early, N):
                 term(b, seq[i], i == 0, i == N - 1)
@@ -376,7 +417,7 @@ def rank_program(g, core, T, topo):
 
         before("g", ["qh"])
         e = wide(me)
-        at = [Q * ((dests(d).index(me) + 1) % 3) for d in order[:3]]
+        at = [slot_h(me, d) for d in order[:3]]
         aH = "aH%d_%d" % (t, me)
         g.remote_dma_fused([RemoteDMATransfer(dst_ids=[dst_id(d) for d in order[:3]], dma_engine_mask=_bits(e),
                                               remote_sem=T.sem[aH], srcs=[T.qhs[:, 0:Q]],
@@ -387,14 +428,14 @@ def rank_program(g, core, T, topo):
         for k, r in enumerate(order[:3]):
             arrive("aH%d_%d" % (t, r), len(wide(r)) + len(topo.engines(cores[r], core)), ["lh%d" % k])
 
-        def add(bk, b, k, n, key):
+        def add(bk, b, k):
             s = 4 * (PAD + Q * k) + b
-            op("v", "tt", (T.sp[:, C * b + Q * k:C * b + Q * (k + n)], bank(bk, Q * n), T.ss[:, s:s + 4 * Q * n:4], A.add),
-               r=["s%s%d" % (q, i) for q in "va" for i in range(k, k + n)], w=[key], x=["b%d" % bk])
+            op("v", "tt", (T.sp[:, C * b + Q * k:C * b + Q * (k + 1)], bank(bk, Q), T.ss[:, s:s + 4 * Q:4], A.add),
+               r=["sv%d" % k, "sa%d" % k], w=["p%d_%d" % (k, b)], x=["b%d" % bk])
 
         def back(q, b, a, z, key):
             win = T.sp[:, C * b:C * b + C].indirect(T.iu[:, a:z])
-            out, keys = T.xs[:, 64 * a + b:64 * z:4], ["po%d" % b, "pa%d" % b, "pb%d" % b, "iu"]
+            out, keys = T.xs[:, 64 * a + b:64 * z:4], ["p%d_%d" % (k, b) for k in range(4)] + ["iu"]
             if q == "a":
                 op("a", "act", (out, win, F.Copy), r=keys, w=[key], scale=0.5)
             else:
@@ -402,30 +443,31 @@ def rank_program(g, core, T, topo):
 
         for b in range(4):
             unpack(b, b, 128, T.qh[:], T.qhs[:], ["qh"])
-            add(b, b, 3, 1, "po%d" % b)
-        for b in range(4):
-            unpack(4 + b, b, 2 * Q, T.lh[:, Q:3 * Q], T.lhs[:, Q:3 * Q], ["lh0", "lh1"])
-            add(4 + b, b, 0, 2, "pa%d" % b)
-        for b in range(4):
-            unpack(b, b, 128, T.lh[:, 0:128], T.lhs[:, 0:128], ["lh2"])
-        for b in range(4):
-            add(b, b, 2, 1, "pb%d" % b)
-            if b < 2:
-                back("a", b, 0, K, XK[b])
+            add(b, b, 3)
+        for k in range(3):
+            l, first = Q * (2 - k), 4 * ((k + 1) % 2)
+            for b in range(4):
+                unpack(first + b, b, 128, T.lh[:, l:l + 128], T.lhs[:, l:l + 128], ["lh%d" % k, "hp0", "hp1"])
+            for b in range(4):
+                add(first + b, b, k)
+                if k == 2 and b < 2:
+                    back("a", b, 0, K, XK[b])
         back("v", 2, 0, K, XK[2])
         back("a", 3, BV, K, XK[4])
         back("v", 3, 0, BV, XK[3])
 
-    op("v", "quant", (T.qx[:], T.qxs[:], T.xs[:]), r=XK, w=["qx"])
     for h in range(2):
-        op("p", "mm", (bank(h, H2), T.qv[:], T.qvs[:], T.qx[:, H2 * h:H2 * h + H2], T.qxs[:, H2 * h:H2 * h + H2], True, True),
-           r=["qv", "qx"], w=["b%d" % h])
-    dma("y", T.oc[:], u8(T.qx[:]), "stf", r=["qx"])
-    op("v", "copy", (T.ys[:, 0:H2], bank(0, H2)), w=["y0"], x=["b0"])
-    for k in range(4):
-        dma("a" if k == 0 else "y", T.osc[4 * k:4 * k + 4, :], T.qxs[32 * k:32 * k + 4, :], "stf", r=["qx"])
-    op("a", "act", (T.ys[:, H2:C], bank(1, H2), F.Copy), w=["y1"], x=["b1"])
+        a, z = H2 * h, H2 * h + H2
+        op("v", "quant", (T.qx[:, a:z], T.qxs[:, a:z], T.xs[:, 4 * a:4 * z]), r=XK, w=QK if h == 0 else ["qx2"])
+        op("p", "mm", (bank(h, H2), T.qv[:], T.qvs[:], T.qx[:, a:z], T.qxs[:, a:z], True, True),
+           r=["qv", "qx0" if h == 0 else "qx2"], w=["b%d" % h])
+    QK = QK + ["qx2"]
+    op("a", "act", (T.ys[:, 0:H2], bank(0, H2), F.Copy), w=["y0"], x=["b0"])
+    op("v", "copy", (T.ys[:, H2:C], bank(1, H2)), w=["y1"], x=["b1"])
+    dma("y", T.oc[:], u8(T.qx[:]), "stf", r=QK)
     dma("a", T.y[:], T.ys[:], "stf", r=["y0", "y1"])
+    for k in range(4):
+        dma("a" if k == 3 else "y", T.osc[4 * k:4 * k + 4, :], T.qxs[32 * k:32 * k + 4, :], "stf", r=QK)
     for s in SEMAPHORES:
         if count.get(s, 0) > known["g"].get(s, 0):
             g.wait_ge(T.sem[s], count[s])

@@ -8,12 +8,13 @@ Q = C // N
 K = C // 16
 H2 = C // 2
 PAD = 128 - Q
-NV = 13
-MID = 16
+VA, VZ = 8, 19
+F1, F0 = 8 * C, 8 * C + 8 * 256
 GV = (12, 4, 8, 10)
 BV = 20
 LOW = 2.0 ** 90
 X4, U8, U16, I32, BF, FP = "float8_e4m3fn_x4", "uint8", "uint16", "int32", "bfloat16", "float32"
+HF = "float16"
 
 _SB = dict(
     xs=(4 * C, BF), us=(512, BF), vs=(512, BF), qx=(C, X4), qxs=(C, U8), qu=(128, X4), qus=(128, U8),
@@ -22,7 +23,9 @@ _SB = dict(
     pi=(8, I32), pj=(8, I32), pf=(8, FP), uli=(8, I32), ul=(8, U16),
     t16=(C, FP), t4=(C, BF), jr=(C, BF), jv=(C, BF), cap=(C, FP), rad=(C, FP), keep=(C, BF),
     cap4=(C, BF), rad4=(C, BF), base=(K, FP), am=(C, FP), zz=(C, FP), eq=(C, BF), cr=(C, BF),
-    ck=(K, FP), fl=(K * C, BF), rs=(NV * H2, BF), gg=(K, FP), ll=(K, FP), lk=(K, FP), rk=(K, FP),
+    fl=(F0 + 8 * 128, BF), rs=((VZ - VA) * H2, BF),
+    cu=(1032, HF), cw=(516, HF), dd=(288, BF), tr=(544, BF), su=(544, BF),
+    zs=(5 * K, FP), zo=(5 * K, FP), t5=(5 * K, FP), k1=(5 * K, FP), k2=(5 * K, FP), k5=(5 * K, FP),
     iw=(K, U16), iu=(K, U16), tm=(7 * K, FP), ow=(C, BF), a4=(C, BF), z4=(C, BF), off=(Q, U16), olf=(C, FP),
     ss=(4 * (C + 2 * PAD), BF), qs=(512, X4), qss=(512, U8), ls=(3 * 128, X4), lss=(3 * 128, U8),
     ms=(512, BF), qm=(128, X4), qms=(128, U8), hs=(512, BF), qh=(128, X4), qhs=(128, U8),
@@ -109,6 +112,7 @@ def rank_program(g, core, T, topo):
         call = {"copy": lambda: e.tensor_copy(*args), "tt": lambda: e.tensor_tensor(*args),
                 "ts": lambda: e.tensor_scalar(*args), "scan": lambda: e.tensor_tensor_scan(*args),
                 "set": lambda: e.memset(*args), "quant": lambda: e.quantize_mx(*args),
+                "turn": lambda: e.transpose(*args),
                 "act": lambda: e.activation(*args, **kw), "mm": lambda: e.matmul_mx(*args),
                 "iota": lambda: e.iota(*args, **kw), "sel": lambda: e.affine_select(*args)}[name]
         s = own[q]
@@ -159,18 +163,23 @@ def rank_program(g, core, T, topo):
     op("g", "iota", (T.t4[:], [[0, Q], [1, 4]], 0, 0), w=["t4"], **flag)
     op("g", "iota", (T.jr[:], [[1, C]], -H2, 0), w=["jr"], **flag)
     op("g", "iota", (T.base[:], [[16, K]], 16, 0), w=["base"], **flag)
+    op("g", "iota", (T.base[:, VA:16], [[0, 16 - VA]], 128, 0), w=["base"], **flag)
+    op("g", "iota", (T.base[:, 16:VZ], [[0, VZ - 16]], H2, 0), w=["base"], **flag)
+    op("g", "iota", (T.t5[:], [[0, K], [1, 5]], 0, 0), w=["t5"], **flag)
     op("v", "set", (T.ms[:], 0.0), w=MK)
     op("v", "set", (T.hs[:, 4 * Q:512], 0.0), w=["hpad"])
     op("v", "set", (T.ones[:], 1.0), w=["ones"])
     op("v", "set", (T.ss[:, 0:4 * PAD], 0.0), w=["spad0"])
     op("v", "set", (T.ss[:, 4 * (PAD + C):4 * (2 * PAD + C)], 0.0), w=["spad1"])
-    op("v", "set", (T.gg[:, K - 1:K], 0.0), w=["g%d" % (K - 1)])
+    op("v", "set", (T.zs[:], 0.0), w=["%s%d" % (n, k) for n in "lg" for k in range(K)] + ["ck", "pk0", "pk1", "pk2", "pk3"])
     op("v", "quant", (T.qm[:], T.qms[:], T.ms[:]), r=MK, w=["qm"])
     op("v", "ts", (T.pj[:, 0:1], T.pi[:, 0:1], 15, None, A.bitwise_and), r=["pi"], w=["pj0"])
     op("v", "ts", (T.pj[:, 1:2], T.pi[:, 0:1], 2, 3, A.logical_shift_right, A.bitwise_and), r=["pi"], w=["pj1"])
     op("v", "ts", (T.pj[:, 2:3], T.pi[:, 0:1], 3, None, A.bitwise_and), r=["pi"], w=["pj2"])
+    op("v", "ts", (T.pj[:, 5:6], T.pi[:, 0:1], 4, 1, A.logical_shift_right, A.bitwise_and), r=["pi"], w=["pj5"])
     op("v", "copy", (T.ul[:], T.uli[:]), r=["uli"], w=["ul"])
     op("v", "copy", (T.pf[:, 0:3], T.pj[:, 0:3]), r=["pj0", "pj1", "pj2"], w=["pf"])
+    op("v", "copy", (T.pf[:, 5:6], T.pj[:, 5:6]), r=["pj5"], w=["pf5"])
     op("v", "ts", (T.cap[:], T.t16[:], T.pf[:, 0:1], -LOW, A.not_equal, A.mult), r=["t16", "pf"], w=["cap"])
     op("v", "ts", (T.pf[:, 3:4], T.pf[:, 2:3], float(2 * C), None, A.add), r=["pf"], w=["pf3"])
     op("a", "act", (T.keep[:], T.t16[:], F.Sign), r=["t16"], w=["keep"])
@@ -180,6 +189,10 @@ def rank_program(g, core, T, topo):
        r=["qu", "ul"], w=["qb"])
     op("a", "act", (T.qbs[:, 0:128], T.qus[:, 0:128].indirect(T.ul[:, 0:8]), F.Copy), r=["qu", "ul"], w=["qbs"])
     op("v", "ts", (T.cap4[:], T.t4[:], T.pf[:, 1:2], 0.5, A.is_equal, A.subtract), r=["t4", "pf"], w=["cap4"])
+    op("v", "ts", (T.pf[:, 4:5], T.pf[:, 5:6], -1.0, 1.0, A.mult, A.add), r=["pf5"], w=["pf4"])
+    op("v", "set", (T.dd[:], 0.0), w=["dz"])
+    op("v", "copy", (T.cu[:, 0:8], T.ms[:, 0:8]), r=MK, w=["cz"])
+    op("v", "copy", (T.cw[:, 0:4], T.ms[:, 0:4]), r=MK, w=["cy"])
     op("a", "act", (T.jv[:], T.jr[:], F.Copy), r=["jr"], w=["jv"], scale=1.0 / 512)
     for b in range(4):
         op("g", "sel", (T.es[:, 512 * b:512 * b + 512], T.ones[:], [[1, 512]], A.is_equal, 0.0, -b, -4),
@@ -208,83 +221,128 @@ def rank_program(g, core, T, topo):
             op("p", "mm", (bank(b, C), T.qb[:], T.qbs[:], T.qx[:], T.qxs[:], True, True),
                r=["qb", "qbs"] + QK, w=["b%d" % b])
         span = {0: (top, C, 2), 1: (0, top, 0)}
-        for n in range(2):
+
+        def mask(n):
             a, z, bk = span[n]
             op("v", "tt", (T.am[:, a:z], bank(bk, z - a), T.cap[:, a:z], A.add), r=["cap"], w=["am%d" % n],
                x=["b%d" % bk])
-            if t == 0 and n == 0:
-                op("v", "ts", (T.rad4[:], T.t4[:], 0.5, -2.0, A.is_lt, A.mult), r=["t4"], w=["rad4"])
+
+        def hold(n):
+            a, z, bk = span[n]
             op("v", "scan", (T.zz[:, a:z], T.rad[:, a:z], T.am[:, a:z], 0.0, A.add, A.max),
                r=["rad", "am%d" % n], w=["z%d" % n])
 
+        def flags(c, a, z):
+            q = c // 8
+            if q == 0:
+                return T.fl[:, F0 + 128 * c + a:F0 + 128 * c + z]
+            o = (F1 if q == 1 else 0) + c % 8
+            return T.fl[:, o + 8 * a:o + 8 * (z - 1) + 1:8]
+
         def sign(c):
-            op("a", "act", (T.fl[:, C * c:C * c + C], bank(1, C), F.Sign), r=["z0" if 16 * c >= top else "z1"],
+            e = 128 * (c // 8 + 1)
+            op("a", "act", (flags(c, 0, e), bank(1, e), F.Sign), r=["z0" if 16 * c >= top else "z1"],
                w=["f%d" % c, "h%d" % c], x=["b1"], bias=T.zz[:, 16 * c + 15:16 * c + 16], scale=-1.0)
 
-        def tally(c):
-            m = C * c + 16 * c + 16
-            op("a", "act", (T.fl[:, C * c:m], T.fl[:, C * c:m], F.Relu), r=["f%d" % c], w=["f%d" % c, "l%d" % c],
-               accum_out=T.ll[:, c:c + 1])
-            if c < K - 1:
-                op("a", "act", (T.fl[:, m:C * c + C], T.fl[:, m:C * c + C], F.Relu), r=["h%d" % c],
-                   w=["h%d" % c, "g%d" % c], scale=-1.0, accum_out=T.gg[:, c:c + 1])
+        def below(c):
+            m = 16 * c + 16
+            op("a", "act", (flags(c, 0, m), flags(c, 0, m), F.Relu), r=["f%d" % c], w=["f%d" % c, "l%d" % c],
+               accum_out=T.zs[:, 5 * c:5 * c + 1])
 
-        sign(K - 1)
-        for c in range(K - 1, NV - 1, -1):
-            if c > NV:
-                sign(c - 1)
-            tally(c)
+        def above(c):
+            m, e = 16 * c + 16, 128 * (c // 8 + 1)
+            if m < e:
+                op("a", "act", (flags(c, m, e), flags(c, m, e), F.Relu), r=["h%d" % c],
+                   w=["h%d" % c, "g%d" % c], scale=-1.0, accum_out=T.zs[:, 5 * c + 2:5 * c + 3])
 
         def compare(c):
-            m = 16 * c + 16
-            s = T.zz[:, m - 1:m]
-            op("v", "ts", (T.fl[:, C * c:C * c + m], bank(0, m), s, 0.5, A.is_ge, A.subtract),
-               r=["z1"], w=["f%d" % c], x=["b0"])
-            op("v", "ts", (T.fl[:, C * c + m:C * c + C], bank(0, C - m, m), s, 0.5, A.is_gt, A.subtract),
-               r=["z1"], w=["h%d" % c], x=["b0"])
+            m, e = 16 * c + 16, 128 * (c // 8 + 1)
+            s, zk = T.zz[:, m - 1:m], "z0" if 16 * c >= top else "z1"
+            op("v", "ts", (flags(c, 0, m), bank(0, m), s, None, A.is_lt), r=[zk], w=["f%d" % c], x=["b0"])
+            if m < e:
+                op("v", "ts", (flags(c, m, e), bank(0, e - m, m), s, None, A.is_le), r=[zk], w=["h%d" % c], x=["b0"])
+
+        def total(c):
+            h, z = 64 * (c // 8 + 1), H2 * (c - VA + 1)
+            op("v", "scan", (T.rs[:, z - h:z], flags(c, 0, h), flags(c, h, 2 * h), float(-h), A.add, A.add),
+               r=["f%d" % c, "h%d" % c], w=["r%d" % c])
 
         def place(a, z, keys):
             op("v", "copy", (T.ow[:, 0:C].indirect(T.iw[:, a:z]), T.jv[:, 16 * a:16 * z]), r=keys + ["jv"], w=["ow"])
 
-        def lower(a, z):
-            op("v", "tt", (T.lk[:, a:z], T.ck[:, a:z], T.ll[:, a:z], A.subtract),
-               r=["ck"] + ["l%d" % k for k in range(a, z)], w=["lk%d" % a])
-
-        def upper(a, z):
-            op("v", "tt", (T.rk[:, a:z], T.gg[:, a:z], T.lk[:, a:z], A.add),
-               r=["lk%d" % a] + ["g%d" % k for k in range(a, z)], w=["rk%d" % a])
+        def fold(a, z, keys):
+            op("v", "scan", (T.zo[:, 5 * a:5 * z], T.k5[:, 5 * a:5 * z], T.zs[:, 5 * a:5 * z], 0.0, A.mult, A.add),
+               r=keys + ["ck", "k5"] + ["%s%d" % (n, k) for n in "lg" for k in range(a, z)], w=["rk%d" % a])
 
         def narrow(a, z):
-            op("v", "copy", (T.iw[:, a:z], T.rk[:, a:z]), r=["rk%d" % a], w=["iw%d" % a])
+            op("v", "copy", (T.iw[:, a:z], T.zo[:, 5 * a + 4:5 * z:5]), r=["rk%d" % a], w=["iw%d" % a])
 
-        def single(c):
-            op("v", "ts", (T.iw[:, c:c + 1], T.gg[:, c:c + 1], T.ck[:, c:c + 1], T.ll[:, c:c + 1], A.add, A.subtract),
-               r=["ck", "g%d" % c, "l%d" % c], w=["iw%d" % c])
+        def pick(n, out, in_, key):
+            s = T.pf[:, 4 + n % 2:5 + n % 2]
+            op("v", "ts", (out, in_, s, None, A.mult), r=[key, "pf4", "pf5"], w=["pk%d" % n])
 
-        op("v", "tt", (T.eq[:], bank(0, C), T.zz[:], A.is_equal), r=["z0", "z1"], w=["eq"], x=["b0"])
-        compare(0)
+        mask(0)
+        if t == 0:
+            op("v", "ts", (T.rad4[:], T.t4[:], 0.5, -2.0, A.is_lt, A.mult), r=["t4"], w=["rad4"])
+        hold(0)
+        mask(1)
+        compare(16)
+        hold(1)
+        sign(K - 1)
+        for c in range(K - 1, VZ, -1):
+            sign(c - 1)
+            below(c)
+            if c > VZ + 1:
+                above(c)
+        sign(VA - 1)
+        below(VZ)
+        above(VZ + 1)
+        above(VZ)
+        for c in range(VA - 1, -1, -1):
+            if c > 0:
+                sign(c - 1)
+            below(c)
+            above(c)
+        rows = list(range(16, VZ)) + list(range(VA, 16))
+        for i, c in enumerate(rows):
+            if i + 1 < len(rows):
+                compare(rows[i + 1])
+            else:
+                op("v", "tt", (T.eq[:], bank(0, C), T.zz[:], A.is_equal), r=["z0", "z1"], w=["eq"], x=["b0"])
+            total(c)
+        if t == 0:
+            op("v", "ts", (T.k1[:], T.t5[:], 1.0, -2.0, A.is_equal, A.mult), r=["t5"], w=["k1"])
+            op("v", "ts", (T.k2[:], T.t5[:], 0.5, None, A.is_gt), r=["t5"], w=["k2"])
+        FK = ["f%d" % c for c in range(K)]
+        op("v", "scan", (T.cw[:, 4:516], T.fl[:, 1024:2048:2], T.fl[:, 1025:2048:2], 0.0, A.add, A.add),
+           r=FK[16:] + ["cy"], w=["cu1"])
+        op("v", "scan", (T.cu[:, 8:1032], T.fl[:, 0:1024], T.fl[:, F1:F1 + 1024], 0.0, A.add, A.add),
+           r=FK[8:] + ["cz"], w=["cu0"])
+        if t == 0:
+            op("v", "tt", (T.k5[:], T.k1[:], T.k2[:], A.add), r=["k1", "k2"], w=["k5"])
+        op("v", "scan", (T.dd[:, 144:272], T.cw[:, 7:516:4], T.cw[:, 3:512:4], 0.0, A.max, A.subtract),
+           r=["cu1", "dz"], w=["d1"])
         op("v", "scan", (T.cr[:], T.keep[:], T.eq[:], 0.0, A.mult, A.subtract), r=["keep", "eq"], w=["cr"])
-        for c in range(NV):
-            if c + 1 < NV:
-                compare(c + 1)
-            if c == 0:
-                op("v", "tt", (T.ck[:], T.cr[:, 15:C:16], T.base[:], A.add), r=["cr", "base"], w=["ck"])
-            if c == NV - 1:
-                lower(MID, K)
-            op("v", "scan", (T.rs[:, H2 * c:H2 * c + H2], T.fl[:, C * c:C * c + H2], T.fl[:, C * c + H2:C * c + C],
-                             T.cr[:, 16 * c + 15:16 * c + 16], A.add, A.add), r=["f%d" % c, "h%d" % c, "cr"], w=["r%d" % c])
-        even = NV - NV % 2
-        IK = ["iw0", "iw%d" % MID] + ["iw%d" % c for c in range(NV, MID)]
-        upper(MID, K)
-        op("v", "ts", (T.iw[:, 0:NV], T.rs[:, H2 - 1:H2 * NV:H2], float(H2), None, A.add),
-           r=["r%d" % k for k in range(NV)], w=["iw0"])
-        narrow(MID, K)
-        place(0, even, IK[:1])
-        single(MID - 1)
-        place(MID, K, IK[1:2])
-        for c in range(MID - 2, NV - 1, -1):
-            single(c)
-        place(even, MID, IK)
+        op("v", "scan", (T.dd[:, 16:144], T.cu[:, 15:1032:8], T.cu[:, 7:1024:8], 0.0, A.max, A.subtract),
+           r=["cu0", "dz"], w=["d0"])
+        op("v", "copy", (T.zs[:, 5 * VA:5 * VZ:5], T.rs[:, H2 - 1:H2 * (VZ - VA):H2]),
+           r=["r%d" % k for k in range(VA, VZ)], w=["l%d" % k for k in range(VA, VZ)])
+        op("v", "tt", (T.zs[:, 1:5 * K:5], T.cr[:, 15:C:16], T.base[:], A.add), r=["cr", "base"], w=["ck"])
+        op("v", "turn", (T.tr[:, 0:256], T.dd[:, 16:272]), r=["d0", "d1"], w=["t0"])
+        op("v", "turn", (T.tr[:, 256:544], T.dd[:, 0:288]), r=["d0", "d1"], w=["t1"])
+        fold(16, K, [])
+        op("v", "scan", (T.su[:, 0:256], T.keep[:, 0:256], T.tr[:, 0:256], 0.0, A.mult, A.add), r=["t0"], w=["s0"])
+        op("v", "scan", (T.su[:, 256:544], T.keep[:, 0:288], T.tr[:, 256:544], 0.0, A.mult, A.add), r=["t1"], w=["s1"])
+        narrow(16, K)
+        pick(0, T.zs[:, 3:80:10], T.su[:, 15:256:32], "s0")
+        pick(1, T.zs[:, 9:80:10], T.su[:, 31:256:32], "s0")
+        pick(2, T.zs[:, 8:80:10], T.su[:, 256 + 47:544:32], "s1")
+        pick(3, T.zs[:, 4:80:10], T.su[:, 256 + 31:512:32], "s1")
+        place(16, K, ["iw16"])
+        fold(0, 16, ["pk0", "pk1", "pk2", "pk3"])
+        narrow(0, 16)
+        IK = ["iw0", "iw16"]
+        place(0, 16, IK)
 
         def lay(step, qs):
             a, z = Q * min(qs), Q * (max(qs) + 1)

@@ -1,4 +1,3 @@
-from concourse.bass import DstId, RemoteDMATransfer
 from concourse.mybir import dt, AluOpType, ActivationFunctionType
 
 A = AluOpType
@@ -10,7 +9,7 @@ H2 = C // 2
 PAD = 128 - Q
 VA, VZ = 8, 19
 F1, F0 = 8 * C, 8 * C + 8 * 256
-GV = (12, 4, 8, 10)
+GV = (12, 8, 8, 12)
 BV = 20
 LOW = 2.0 ** 90
 X4, U8, U16, I32, BF, FP = "float8_e4m3fn_x4", "uint8", "uint16", "int32", "bfloat16", "float32"
@@ -22,17 +21,17 @@ _SB = dict(
     ones=(512, BF), es=(2048, BF), qe=(512, X4), qes=(512, U8),
     pi=(8, I32), pj=(8, I32), pf=(8, FP), uli=(8, I32), ul=(8, U16),
     t16=(C, FP), t4=(C, BF), jr=(C, BF), jv=(C, BF), cap=(C, FP), rad=(C, FP), keep=(C, BF),
-    cap4=(C, BF), rad4=(C, BF), base=(K, FP), am=(C, FP), zz=(C, FP), eq=(C, BF), cr=(C, BF),
+    c4=(C, BF), t2=(16, FP), m0=(16, BF), m1=(16, BF), base=(K, FP), am=(C, FP), zz=(C, FP), eq=(C, BF), cr=(C, BF),
     fl=(F0 + 8 * 128, BF), rs=((VZ - VA) * H2, BF),
     cu=(1032, HF), cw=(516, HF), dd=(288, BF), tr=(544, BF), su=(544, BF),
     zs=(5 * K, FP), zo=(5 * K, FP), t5=(5 * K, FP), k1=(5 * K, FP), k2=(5 * K, FP), k5=(5 * K, FP),
-    iw=(K, U16), iu=(K, U16), tm=(7 * K, FP), ow=(C, BF), a4=(C, BF), z4=(C, BF), off=(Q, U16), olf=(C, FP),
+    iw=(K, U16), iu=(K, U16), tm=(7 * K, FP), ow=(C, BF), z4=(C, HF), off=(Q, U16), olf=(C, FP),
     ss=(4 * (C + 2 * PAD), BF), qs=(512, X4), qss=(512, U8), ls=(3 * 128, X4), lss=(3 * 128, U8),
     ms=(512, BF), qm=(128, X4), qms=(128, U8), hs=(512, BF), qh=(128, X4), qhs=(128, U8),
     lh=(3 * Q + PAD, X4), lhs=(3 * Q + PAD, U8), sp=(4 * C, FP), ys=(C, FP))
 SCRATCH = {n: ("sbuf", [128, w], d) for n, (w, d) in _SB.items()}
 SCRATCH["ps"] = ("psum", [128, 8 * 512], FP)
-SEMAPHORES = (["sv", "sa", "sp", "sg", "ldx", "ldu", "ldw", "ldp", "sto", "stf"]
+SEMAPHORES = (["sv", "sa", "sp", "sg", "ldx", "ldz", "ldu", "ldw", "ldp", "sto", "stf"]
               + ["%s%d" % (n, t) for n in ("lS", "lH") for t in range(R)]
               + ["%s%d_%d" % (n, t, r) for n in ("aS", "aH") for t in range(R) for r in range(N)])
 
@@ -40,10 +39,6 @@ SEMAPHORES = (["sv", "sa", "sp", "sg", "ldx", "ldu", "ldw", "ldp", "sto", "stf"]
 def _near(topo, a, b):
     ca, cb = topo.chip(a), topo.chip(b)
     return 2 if topo.mates(ca, cb) else 1 if topo.same_plane(ca, cb) else 0
-
-
-def _bits(engines):
-    return sum(1 << e for e in engines)
 
 
 def rank_program(g, core, T, topo):
@@ -57,18 +52,6 @@ def rank_program(g, core, T, topo):
 
     def dests(r):
         return sorted(others(r), key=lambda d: (_near(topo, cores[r], cores[d]), d))
-
-    def dst_id(d):
-        rid, pid, _ = topo.addr(cores[d])
-        return DstId(rid=rid, pnc=pid)
-
-    def halves(r, d):
-        e = topo.engines(cores[r], cores[d])
-        return e[:len(e) // 2], e[len(e) // 2:]
-
-    def wide(r):
-        e = [set(topo.engines(cores[r], cores[d])) for d in others(r)]
-        return sorted(e[0] & e[1] & e[2])
 
     def slot_s(r, d):
         return 128 * others(d).index(r)
@@ -150,62 +133,59 @@ def rank_program(g, core, T, topo):
         return v.bitcast(dt.uint8)
 
     XK = ["x0", "x1", "x2", "x3", "x4"]
-    MK = ["m0", "m1", "m2", "m3"]
+    XR = ["xr0", "xr1"]
+    MK = ["ms0", "ms1", "ms2", "ms3"]
     flag = dict(allow_small_or_imprecise_dtypes=True)
 
     dma("a", T.us[:], T.u[:], "ldu", w=["us"])
-    dma("y", T.xs[:, 0:2 * C], T.x[:, 0:2 * C], "ldx", w=XK[:2])
-    dma("a", T.xs[:, 2 * C:4 * C], T.x[:, 2 * C:4 * C], "ldx", w=XK[2:])
+    dma("y", T.xs[:, 1024:4 * C], T.x[:, 1024:4 * C], "ldx", w=["xt"])
+    dma("y", T.xs[:, 0:512], T.x[:, 0:512], "ldz", w=["xr0"])
+    dma("a", T.xs[:, 512:1024], T.x[:, 512:1024], "ldz", w=["xr1"])
 
-    op("g", "iota", (T.t16[:], [[0, K], [1, 16]], 0, 0), w=["t16"], **flag)
     op("g", "iota", (T.pi[:, 0:1], [[0, 1]], 0, 1), w=["pi"])
     op("g", "iota", (T.uli[:], [[16, 8]], 0, 0), w=["uli"])
+    op("g", "iota", (T.t16[:], [[0, K], [1, 16]], 0, 0), w=["t16"], **flag)
+    op("g", "iota", (T.t5[:], [[0, K], [1, 5]], 0, 0), w=["t5"], **flag)
+    op("g", "iota", (T.t2[:], [[0, 8], [1, 2]], 0, 0), w=["t2"], **flag)
     op("g", "iota", (T.t4[:], [[0, Q], [1, 4]], 0, 0), w=["t4"], **flag)
     op("g", "iota", (T.jr[:], [[1, C]], -H2, 0), w=["jr"], **flag)
     op("g", "iota", (T.base[:], [[16, K]], 16, 0), w=["base"], **flag)
     op("g", "iota", (T.base[:, VA:16], [[0, 16 - VA]], 128, 0), w=["base"], **flag)
     op("g", "iota", (T.base[:, 16:VZ], [[0, VZ - 16]], H2, 0), w=["base"], **flag)
-    op("g", "iota", (T.t5[:], [[0, K], [1, 5]], 0, 0), w=["t5"], **flag)
-    op("v", "set", (T.ms[:], 0.0), w=MK)
-    op("v", "set", (T.hs[:, 4 * Q:512], 0.0), w=["hpad"])
     op("v", "set", (T.ones[:], 1.0), w=["ones"])
-    op("v", "set", (T.ss[:, 0:4 * PAD], 0.0), w=["spad0"])
-    op("v", "set", (T.ss[:, 4 * (PAD + C):4 * (2 * PAD + C)], 0.0), w=["spad1"])
-    op("v", "set", (T.zs[:], 0.0), w=["%s%d" % (n, k) for n in "lg" for k in range(K)] + ["ck", "pk0", "pk1", "pk2", "pk3"])
-    op("v", "quant", (T.qm[:], T.qms[:], T.ms[:]), r=MK, w=["qm"])
+    op("v", "set", (T.zs[:], 0.0), w=["%s%d" % (n, k) for n in "lg" for k in range(K)] + ["ck", "pk0", "pk1"])
+    op("v", "set", (T.dd[:], 0.0), w=["dz"])
     op("v", "ts", (T.pj[:, 0:1], T.pi[:, 0:1], 15, None, A.bitwise_and), r=["pi"], w=["pj0"])
     op("v", "ts", (T.pj[:, 1:2], T.pi[:, 0:1], 2, 3, A.logical_shift_right, A.bitwise_and), r=["pi"], w=["pj1"])
     op("v", "ts", (T.pj[:, 2:3], T.pi[:, 0:1], 3, None, A.bitwise_and), r=["pi"], w=["pj2"])
-    op("v", "ts", (T.pj[:, 5:6], T.pi[:, 0:1], 4, 1, A.logical_shift_right, A.bitwise_and), r=["pi"], w=["pj5"])
+    op("v", "ts", (T.pj[:, 3:4], T.pi[:, 0:1], 4, 1, A.logical_shift_right, A.bitwise_and), r=["pi"], w=["pj3"])
     op("v", "copy", (T.ul[:], T.uli[:]), r=["uli"], w=["ul"])
-    op("v", "copy", (T.pf[:, 0:3], T.pj[:, 0:3]), r=["pj0", "pj1", "pj2"], w=["pf"])
-    op("v", "copy", (T.pf[:, 5:6], T.pj[:, 5:6]), r=["pj5"], w=["pf5"])
+    op("v", "copy", (T.pf[:, 0:4], T.pj[:, 0:4]), r=["pj0", "pj1", "pj2", "pj3"], w=["pf"])
+    op("v", "copy", (T.cu[:, 0:8], T.dd[:, 0:8]), r=["dz"], w=["cz"])
+    op("v", "copy", (T.cw[:, 0:4], T.dd[:, 0:4]), r=["dz"], w=["cy"])
     op("v", "ts", (T.cap[:], T.t16[:], T.pf[:, 0:1], -LOW, A.not_equal, A.mult), r=["t16", "pf"], w=["cap"])
-    op("v", "ts", (T.pf[:, 3:4], T.pf[:, 2:3], float(2 * C), None, A.add), r=["pf"], w=["pf3"])
+    op("a", "act", (T.ms[:], T.ones[:], F.Copy), r=["ones"], w=MK, scale=0.0)
     op("a", "act", (T.keep[:], T.t16[:], F.Sign), r=["t16"], w=["keep"])
     op("a", "act", (T.rad[:], T.keep[:], F.Identity), r=["keep"], w=["rad"], scale=4 * LOW, bias=-4 * LOW)
+    op("v", "ts", (T.pf[:, 4:5], T.pf[:, 1:2], -2048.0, T.pf[:, 2:3], A.mult, A.add), r=["pf"], w=["pf4"])
+    op("v", "ts", (T.k1[:], T.t5[:], 1.0, -2.0, A.is_equal, A.mult), r=["t5"], w=["k1"])
+    op("v", "ts", (T.k2[:], T.t5[:], 0.5, None, A.is_gt), r=["t5"], w=["k2"])
     op("v", "quant", (T.qu[:], T.qus[:], T.us[:]), r=["us"], w=["qu"])
+    op("v", "ts", (T.pf[:, 5:6], T.pf[:, 4:5], float(2 * C + 3 * 2048), None, A.add), r=["pf4"], w=["pf5"])
     op("v", "copy", (T.qb[:, 0:128].bitcast(dt.uint32), T.qu[:, 0:128].bitcast(dt.uint32).indirect(T.ul[:, 0:8])),
        r=["qu", "ul"], w=["qb"])
     op("a", "act", (T.qbs[:, 0:128], T.qus[:, 0:128].indirect(T.ul[:, 0:8]), F.Copy), r=["qu", "ul"], w=["qbs"])
-    op("v", "ts", (T.cap4[:], T.t4[:], T.pf[:, 1:2], 0.5, A.is_equal, A.subtract), r=["t4", "pf"], w=["cap4"])
-    op("v", "ts", (T.pf[:, 4:5], T.pf[:, 5:6], -1.0, 1.0, A.mult, A.add), r=["pf5"], w=["pf4"])
-    op("v", "set", (T.dd[:], 0.0), w=["dz"])
-    op("v", "copy", (T.cu[:, 0:8], T.ms[:, 0:8]), r=MK, w=["cz"])
-    op("v", "copy", (T.cw[:, 0:4], T.ms[:, 0:4]), r=MK, w=["cy"])
-    op("a", "act", (T.jv[:], T.jr[:], F.Copy), r=["jr"], w=["jv"], scale=1.0 / 512)
+    for key, view in (("spad0", T.ss[:, 0:4 * PAD]), ("spad1", T.ss[:, 4 * (PAD + C):4 * (2 * PAD + C)]),
+                      ("hpad", T.hs[:, 4 * Q:512])):
+        op("a", "act", (view, T.ones[:, 0:4 * PAD], F.Copy), r=["ones"], w=[key], scale=0.0)
+    op("a", "act", (T.jv[:], T.jr[:], F.Copy), r=["jr"], w=["jv"], scale=1.0 / 4096)
     for b in range(4):
         op("g", "sel", (T.es[:, 512 * b:512 * b + 512], T.ones[:], [[1, 512]], A.is_equal, 0.0, -b, -4),
            r=["ones"], w=["e%d" % b])
-    wait("y", [writer["x0"]])
+    wait("y", [writer["xr0"]])
     dma("y", u8(T.qw[:]), T.wc[:], "ldw", w=["qw"])
     dma("y", T.qws[:], T.ws[:], "ldw", w=["qw2"])
     dma("y", T.vs[:], T.v[:], "ldw", w=["vs"])
-    for i in range(3):
-        dma("y", u8(T.ls[:, 128 * i + Q:128 * i + 128]), u8(T.qm[:, 0:PAD]), "ldp", r=["qm"], w=["lpad%d" % i])
-        dma("y", T.lss[:, 128 * i + Q:128 * i + 128], T.qms[:, 0:PAD], "ldp", r=["qm"], w=["lspad%d" % i])
-    dma("y", u8(T.lh[:, 3 * Q:3 * Q + PAD]), u8(T.qm[:, 0:PAD]), "ldp", r=["qm"], w=["hp0"])
-    dma("y", T.lhs[:, 3 * Q:3 * Q + PAD], T.qms[:, 0:PAD], "ldp", r=["qm"], w=["hp1"])
 
     order = dests(me) + [me]
     shift = [Q * (order.index(q) - q) for q in range(N)]
@@ -213,13 +193,9 @@ def rank_program(g, core, T, topo):
     QK = ["qx0", "qx1"]
 
     for t in range(R):
-        op("v", "quant", (T.qx[:, top:C], T.qxs[:, top:C], T.xs[:, 4 * top:4 * C]), r=XK, w=["qx0"])
+        op("v", "quant", (T.qx[:, top:C], T.qxs[:, top:C], T.xs[:, 4 * top:4 * C]), r=XK + ["xt"], w=["qx0"])
         op("p", "mm", (bank(2, C - top), T.qb[:], T.qbs[:], T.qx[:, top:C], T.qxs[:, top:C], True, True),
            r=["qb", "qbs", "qx0"], w=["b2"])
-        op("v", "quant", (T.qx[:, 0:top], T.qxs[:, 0:top], T.xs[:, 0:4 * top]), r=XK, w=["qx1"])
-        for b in range(2):
-            op("p", "mm", (bank(b, C), T.qb[:], T.qbs[:], T.qx[:], T.qxs[:], True, True),
-               r=["qb", "qbs"] + QK, w=["b%d" % b])
         span = {0: (top, C, 2), 1: (0, top, 0)}
 
         def mask(n):
@@ -231,6 +207,19 @@ def rank_program(g, core, T, topo):
             a, z, bk = span[n]
             op("v", "scan", (T.zz[:, a:z], T.rad[:, a:z], T.am[:, a:z], 0.0, A.add, A.max),
                r=["rad", "am%d" % n], w=["z%d" % n])
+
+        if t == 0:
+            op("v", "quant", (T.qm[:], T.qms[:], T.ms[:]), r=MK, w=["qm"])
+            op("v", "tt", (T.k5[:], T.k1[:], T.k2[:], A.add), r=["k1", "k2"], w=["k5"])
+            for i in range(3):
+                dma("y", u8(T.ls[:, 128 * i + Q:128 * i + 128]), u8(T.qm[:, 0:PAD]), "ldp", r=["qm"], w=["lpad%d" % i])
+                dma("y", T.lss[:, 128 * i + Q:128 * i + 128], T.qms[:, 0:PAD], "ldp", r=["qm"], w=["lspad%d" % i])
+            dma("y", u8(T.lh[:, 3 * Q:3 * Q + PAD]), u8(T.qm[:, 0:PAD]), "ldp", r=["qm"], w=["hp0"])
+            dma("y", T.lhs[:, 3 * Q:3 * Q + PAD], T.qms[:, 0:PAD], "ldp", r=["qm"], w=["hp1"])
+        op("v", "quant", (T.qx[:, 0:top], T.qxs[:, 0:top], T.xs[:, 0:4 * top]), r=XK + XR, w=["qx1"])
+        for b in range(2):
+            op("p", "mm", (bank(b, C), T.qb[:], T.qbs[:], T.qx[:], T.qxs[:], True, True),
+               r=["qb", "qbs"] + QK, w=["b%d" % b])
 
         def flags(c, a, z):
             q = c // 8
@@ -277,13 +266,9 @@ def rank_program(g, core, T, topo):
         def narrow(a, z):
             op("v", "copy", (T.iw[:, a:z], T.zo[:, 5 * a + 4:5 * z:5]), r=["rk%d" % a], w=["iw%d" % a])
 
-        def pick(n, out, in_, key):
-            s = T.pf[:, 4 + n % 2:5 + n % 2]
-            op("v", "ts", (out, in_, s, None, A.mult), r=[key, "pf4", "pf5"], w=["pk%d" % n])
-
         mask(0)
         if t == 0:
-            op("v", "ts", (T.rad4[:], T.t4[:], 0.5, -2.0, A.is_lt, A.mult), r=["t4"], w=["rad4"])
+            op("v", "ts", (T.c4[:], T.t4[:], T.pf[:, 1:2], 0.125, A.is_le, A.subtract), r=["t4", "pf"], w=["c4"])
         hold(0)
         mask(1)
         compare(16)
@@ -310,54 +295,48 @@ def rank_program(g, core, T, topo):
             else:
                 op("v", "tt", (T.eq[:], bank(0, C), T.zz[:], A.is_equal), r=["z0", "z1"], w=["eq"], x=["b0"])
             total(c)
-        if t == 0:
-            op("v", "ts", (T.k1[:], T.t5[:], 1.0, -2.0, A.is_equal, A.mult), r=["t5"], w=["k1"])
-            op("v", "ts", (T.k2[:], T.t5[:], 0.5, None, A.is_gt), r=["t5"], w=["k2"])
         FK = ["f%d" % c for c in range(K)]
         op("v", "scan", (T.cw[:, 4:516], T.fl[:, 1024:2048:2], T.fl[:, 1025:2048:2], 0.0, A.add, A.add),
            r=FK[16:] + ["cy"], w=["cu1"])
         op("v", "scan", (T.cu[:, 8:1032], T.fl[:, 0:1024], T.fl[:, F1:F1 + 1024], 0.0, A.add, A.add),
            r=FK[8:] + ["cz"], w=["cu0"])
-        if t == 0:
-            op("v", "tt", (T.k5[:], T.k1[:], T.k2[:], A.add), r=["k1", "k2"], w=["k5"])
         op("v", "scan", (T.dd[:, 144:272], T.cw[:, 7:516:4], T.cw[:, 3:512:4], 0.0, A.max, A.subtract),
            r=["cu1", "dz"], w=["d1"])
-        op("v", "scan", (T.cr[:], T.keep[:], T.eq[:], 0.0, A.mult, A.subtract), r=["keep", "eq"], w=["cr"])
         op("v", "scan", (T.dd[:, 16:144], T.cu[:, 15:1032:8], T.cu[:, 7:1024:8], 0.0, A.max, A.subtract),
            r=["cu0", "dz"], w=["d0"])
+        op("v", "scan", (T.cr[:], T.keep[:], T.eq[:], 0.0, A.mult, A.subtract), r=["keep", "eq"], w=["cr"])
+        op("v", "turn", (T.tr[:, 0:256], T.dd[:, 16:272]), r=["d0", "d1"], w=["t0"])
+        op("v", "turn", (T.tr[:, 256:544], T.dd[:, 0:288]), r=["d0", "d1"], w=["t1"])
         op("v", "copy", (T.zs[:, 5 * VA:5 * VZ:5], T.rs[:, H2 - 1:H2 * (VZ - VA):H2]),
            r=["r%d" % k for k in range(VA, VZ)], w=["l%d" % k for k in range(VA, VZ)])
         op("v", "tt", (T.zs[:, 1:5 * K:5], T.cr[:, 15:C:16], T.base[:], A.add), r=["cr", "base"], w=["ck"])
-        op("v", "turn", (T.tr[:, 0:256], T.dd[:, 16:272]), r=["d0", "d1"], w=["t0"])
-        op("v", "turn", (T.tr[:, 256:544], T.dd[:, 0:288]), r=["d0", "d1"], w=["t1"])
-        fold(16, K, [])
         op("v", "scan", (T.su[:, 0:256], T.keep[:, 0:256], T.tr[:, 0:256], 0.0, A.mult, A.add), r=["t0"], w=["s0"])
-        op("v", "scan", (T.su[:, 256:544], T.keep[:, 0:288], T.tr[:, 256:544], 0.0, A.mult, A.add), r=["t1"], w=["s1"])
+        fold(16, K, [])
+        op("v", "scan", (T.su[:, 256:528], T.keep[:, 0:272], T.tr[:, 256:528], 0.0, A.mult, A.add), r=["t1"], w=["s1"])
+        if t == 0:
+            op("v", "ts", (T.m0[:], T.t2[:], T.pf[:, 3:4], None, A.is_equal), r=["t2", "pf"], w=["m0"])
+            op("v", "ts", (T.m1[:], T.t2[:], T.pf[:, 3:4], None, A.not_equal), r=["t2", "pf"], w=["m1"])
+        op("v", "tt", (T.zs[:, 3:80:5], T.su[:, 15:256:16], T.m0[:], A.mult), r=["s0", "m0"], w=["pk0"])
+        op("v", "tt", (T.zs[:, 4:80:5], T.su[:, 256 + 31:528:16], T.m1[:], A.mult), r=["s1", "m1"], w=["pk1"])
         narrow(16, K)
-        pick(0, T.zs[:, 3:80:10], T.su[:, 15:256:32], "s0")
-        pick(1, T.zs[:, 9:80:10], T.su[:, 31:256:32], "s0")
-        pick(2, T.zs[:, 8:80:10], T.su[:, 256 + 47:544:32], "s1")
-        pick(3, T.zs[:, 4:80:10], T.su[:, 256 + 31:512:32], "s1")
+        fold(0, 16, ["pk0", "pk1"])
         place(16, K, ["iw16"])
-        fold(0, 16, ["pk0", "pk1", "pk2", "pk3"])
         narrow(0, 16)
         IK = ["iw0", "iw16"]
         place(0, 16, IK)
 
-        def lay(step, qs):
-            a, z = Q * min(qs), Q * (max(qs) + 1)
-            ka, kz, ko = ["a4%d" % q for q in qs], ["z4%d" % q for q in qs], ["off%d" % q for q in qs]
+        def lay(step, h):
+            a, z = H2 * h, H2 * h + H2
             if step == 0:
-                op("v", "scan", (T.a4[:, a:z], T.ow[:, a:z], T.cap4[:, a:z], -1.0, A.max, A.min), r=["ow", "cap4"], w=ka)
-            elif step == 1:
-                op("v", "scan", (T.z4[:, a:z], T.rad4[:, a:z], T.a4[:, a:z], 0.0, A.add, A.max), r=["rad4"] + ka, w=kz)
+                op("v", "scan", (T.z4[:, a:z], T.c4[:, a:z], T.ow[:, a:z], 0.0, A.add, A.min), r=["ow", "c4"],
+                   w=["z4%d" % h])
             else:
-                op("v", "ts", (T.off[:, a // 4:z // 4], T.z4[:, a + 3:z:4], 2048.0, T.pf[:, 3:4], A.mult, A.add),
-                   r=kz + ["pf3"], w=ko)
+                op("v", "ts", (T.off[:, a // 4:z // 4], T.z4[:, a + 3:z:4], 16384.0, T.pf[:, 5:6], A.mult, A.add),
+                   r=["z4%d" % h, "pf5"], w=["off%d" % h])
 
         def gather(q, k):
             o, s, n = K * order[k], 4 * (PAD + Q * k), GV[k]
-            keys = XK + ["off%d" % order[k]]
+            keys = XK + XR + ["xt", "off%d" % (order[k] // 2)]
             if q == "v":
                 op("v", "copy", (T.ss[:, s:s + 16 * n], T.xs[:, 0:4 * C].indirect(T.off[:, o:o + n])),
                    r=keys, w=["sv%d" % k])
@@ -373,68 +352,45 @@ def rank_program(g, core, T, topo):
 
         lS, aS, lH = "lS%d" % t, "aS%d_%d" % (t, me), "lH%d" % t
 
-        def ends(k, codes):
-            s, l = 128 * k + PAD, slot_s(me, order[k])
-            if codes:
-                return u8(T.ls[:, l:l + Q]), u8(T.qs[:, s:s + Q])
-            return T.lss[:, l:l + Q], T.qss[:, s:s + Q]
-
-        def write_pair():
-            tr = []
-            for k in range(2):
-                out, in_ = ends(k, False)
-                e = halves(me, order[k])[k]
-                tr.append(RemoteDMATransfer(dst_ids=[dst_id(order[k])], dma_engine_mask=_bits(e), remote_sem=T.sem[aS],
-                                            srcs=[in_], dsts=[out]))
-                shared(lS, "g", len(e), ["qs%d" % k])
-            g.remote_dma_fused(tr, local_sem=T.sem[lS])
-
         def leave(k):
+            s, l = 128 * k + PAD, slot_s(me, order[k])
             pack(k)
-            send(order[k], *ends(k, True), aS, lS, "qs%d" % k)
+            send(order[k], u8(T.ls[:, l:l + Q]), u8(T.qs[:, s:s + Q]), aS, lS, "qs%d" % k)
+            send(order[k], T.lss[:, l:l + Q], T.qss[:, s:s + Q], aS, lS, "qs%d" % k)
 
-        runs = [order[0:2]] if abs(order[0] - order[1]) == 1 else [order[0:1], order[1:2]]
-        for qs in runs:
-            for step in range(3):
-                lay(step, qs)
-        gather("a", 0)
-        gather("a", 1)
-        gather("v", 0)
-        lay(0, order[2:3])
-        leave(0)
-        lay(1, order[2:3])
-        gather("v", 1)
-        lay(2, order[2:3])
-        gather("a", 2)
-        leave(1)
-        write_pair()
-        gather("v", 2)
-        lay(0, order[3:4])
-        leave(2)
-        send(order[2], *ends(2, False), aS, lS, "qs2")
-        lay(1, order[3:4])
-        lay(2, order[3:4])
-        gather("a", 3)
+        h = order[0] // 2
+        lay(0, h)
+        lay(0, 1 - h)
+        lay(1, h)
+        lay(1, 1 - h)
+        for k in range(N):
+            gather("a", k)
+        for k in range(N - 1):
+            gather("v", k)
+            leave(k)
         gather("v", 3)
         pack(3)
         for r in others(me):
-            k, full = dests(r).index(me), len(topo.engines(cores[r], core))
-            arrive("aS%d_%d" % (t, r), full + (full if k == 2 else len(halves(r, me)[k])), ["ls%d" % r])
+            arrive("aS%d_%d" % (t, r), 2 * len(topo.engines(cores[r], core)), ["ls%d" % r])
 
         if t == 0:
             op("v", "quant", (T.qe[:], T.qes[:], T.es[:]), r=["e0", "e1", "e2", "e3"], w=["qe"])
-            op("v", "quant", (T.qv[:], T.qvs[:], T.vs[:]), r=["vs"], w=["qv"])
         tm = [T.tm[:, K * i:K * i + K] for i in range(7)]
-        for q in range(1, N):
-            op("v", "ts", (tm[q - 1], T.iw[:], float(Q * q), float(shift[q] - shift[q - 1]), A.is_ge, A.mult),
-               r=IK, w=["tm%d" % (q - 1)])
-        op("v", "ts", (tm[3], T.iw[:], float(shift[0]), None, A.add), r=IK, w=["tm3"])
-        op("v", "tt", (tm[4], tm[0], tm[1], A.add), r=["tm0", "tm1"], w=["tm4"])
-        op("v", "tt", (tm[5], tm[2], tm[3], A.add), r=["tm2", "tm3"], w=["tm5"])
-        op("v", "tt", (tm[6], tm[4], tm[5], A.add), r=["tm4", "tm5"], w=["tm6"])
-        op("v", "copy", (T.iu[:], tm[6]), r=["tm6"], w=["iu"])
+
+        def slots():
+            for q in range(1, N):
+                op("v", "ts", (tm[q - 1], T.iw[:], float(Q * q), float(shift[q] - shift[q - 1]), A.is_ge, A.mult),
+                   r=IK, w=["tm%d" % (q - 1)])
+            op("v", "ts", (tm[3], T.iw[:], float(shift[0]), None, A.add), r=IK, w=["tm3"])
+            op("v", "tt", (tm[4], tm[0], tm[1], A.add), r=["tm0", "tm1"], w=["tm4"])
+            op("v", "tt", (tm[5], tm[2], tm[3], A.add), r=["tm2", "tm3"], w=["tm5"])
+            op("v", "tt", (tm[6], tm[4], tm[5], A.add), r=["tm4", "tm5"], w=["tm6"])
+            op("v", "copy", (T.iu[:], tm[6]), r=["tm6"], w=["iu"])
+
+        if t > 0:
+            slots()
         if t == R - 1:
-            op("v", "ts", (T.olf[:], T.ow[:], 512.0, float(H2), A.mult, A.add), r=["ow"], w=["olf"])
+            op("v", "ts", (T.olf[:], T.ow[:], 4096.0, float(H2), A.mult, A.add), r=["ow"], w=["olf"])
             dma("y", T.ol[:], T.olf[0:128:16, :], "sto", r=["olf"])
 
         def unpack(bk, b, n, codes, scales, keys, start=True, stop=True):
@@ -473,18 +429,13 @@ def rank_program(g, core, T, topo):
                    w=["hs%d" % b], x=["b%d" % (4 + b)])
         op("v", "quant", (T.qh[:], T.qhs[:], T.hs[:]), r=["hs0", "hs1", "hs2", "hs3", "hpad"], w=["qh"])
 
-        before("g", ["qh"])
-        e = wide(me)
-        at = [slot_h(me, d) for d in order[:3]]
         aH = "aH%d_%d" % (t, me)
-        g.remote_dma_fused([RemoteDMATransfer(dst_ids=[dst_id(d) for d in order[:3]], dma_engine_mask=_bits(e),
-                                              remote_sem=T.sem[aH], srcs=[T.qhs[:, 0:Q]],
-                                              dsts=[T.lhs[:, l:l + Q] for l in at])], local_sem=T.sem[lH])
-        shared(lH, "g", len(e), ["qh"])
-        for d, l in zip(order[:3], at):
+        for d in order[:3]:
+            l = slot_h(me, d)
             send(d, u8(T.lh[:, l:l + Q]), u8(T.qh[:, 0:Q]), aH, lH, "qh")
+            send(d, T.lhs[:, l:l + Q], T.qhs[:, 0:Q], aH, lH, "qh")
         for k, r in enumerate(order[:3]):
-            arrive("aH%d_%d" % (t, r), len(wide(r)) + len(topo.engines(cores[r], core)), ["lh%d" % k])
+            arrive("aH%d_%d" % (t, r), 2 * len(topo.engines(cores[r], core)), ["lh%d" % k])
 
         def add(bk, b, k):
             s = 4 * (PAD + Q * k) + b
@@ -502,6 +453,9 @@ def rank_program(g, core, T, topo):
         for b in range(4):
             unpack(b, b, 128, T.qh[:], T.qhs[:], ["qh"])
             add(b, b, 3)
+        if t == 0:
+            slots()
+            op("v", "quant", (T.qv[:], T.qvs[:], T.vs[:]), r=["vs"], w=["qv"])
         for k in range(3):
             l, first = Q * (2 - k), 4 * ((k + 1) % 2)
             for b in range(4):
@@ -516,14 +470,16 @@ def rank_program(g, core, T, topo):
 
     for h in range(2):
         a, z = H2 * h, H2 * h + H2
+        key = "qx0" if h == 0 else "qx2"
         op("v", "quant", (T.qx[:, a:z], T.qxs[:, a:z], T.xs[:, 4 * a:4 * z]), r=XK, w=QK if h == 0 else ["qx2"])
         op("p", "mm", (bank(h, H2), T.qv[:], T.qvs[:], T.qx[:, a:z], T.qxs[:, a:z], True, True),
-           r=["qv", "qx0" if h == 0 else "qx2"], w=["b%d" % h])
+           r=["qv", key], w=["b%d" % h])
+        dma("y", T.oc[:, 4 * a:4 * z], u8(T.qx[:, a:z]), "stf", r=[key])
     QK = QK + ["qx2"]
     op("a", "act", (T.ys[:, 0:H2], bank(0, H2), F.Copy), w=["y0"], x=["b0"])
     op("v", "copy", (T.ys[:, H2:C], bank(1, H2)), w=["y1"], x=["b1"])
-    dma("y", T.oc[:], u8(T.qx[:]), "stf", r=QK)
-    dma("a", T.y[:], T.ys[:], "stf", r=["y0", "y1"])
+    dma("a", T.y[:, 0:H2], T.ys[:, 0:H2], "stf", r=["y0"])
+    dma("a", T.y[:, H2:C], T.ys[:, H2:C], "stf", r=["y1"])
     for k in range(4):
         dma("a" if k == 3 else "y", T.osc[4 * k:4 * k + 4, :], T.qxs[32 * k:32 * k + 4, :], "stf", r=QK)
     for s in SEMAPHORES:

from concourse.mybir import dt, AluOpType, ActivationFunctionType

A = AluOpType
F = ActivationFunctionType
C, R, N = 384, 3, 4
Q = C // N
K = C // 16
H2 = C // 2
PAD = 128 - Q
VA, VZ = 8, 19
F1, F0 = 8 * C, 8 * C + 8 * 256
GV = (12, 8, 8, 12)
BV = 20
LOW = 2.0 ** 90
X4, U8, U16, I32, BF, FP = "float8_e4m3fn_x4", "uint8", "uint16", "int32", "bfloat16", "float32"
HF = "float16"

_SB = dict(
    xs=(4 * C, BF), us=(512, BF), vs=(512, BF), qx=(C, X4), qxs=(C, U8), qu=(128, X4), qus=(128, U8),
    qb=(128, X4), qbs=(128, U8), qv=(128, X4), qvs=(128, U8), qw=(512, X4), qws=(512, U8),
    ones=(512, BF), es=(2048, BF), qe=(512, X4), qes=(512, U8),
    pi=(8, I32), pj=(8, I32), pf=(8, FP), uli=(8, I32), ul=(8, U16),
    t16=(C, FP), t4=(C, BF), jr=(C, BF), jv=(C, BF), cap=(C, FP), rad=(C, FP), keep=(C, BF),
    c4=(C, BF), t2=(16, FP), m0=(16, BF), m1=(16, BF), base=(K, FP), am=(C, FP), zz=(C, FP), eq=(C, BF), cr=(C, BF),
    fl=(F0 + 8 * 128, BF), rs=((VZ - VA) * H2, BF),
    cu=(1032, HF), cw=(516, HF), dd=(288, BF), tr=(544, BF), su=(544, BF),
    zs=(5 * K, FP), zo=(5 * K, FP), t5=(5 * K, FP), k1=(5 * K, FP), k2=(5 * K, FP), k5=(5 * K, FP),
    iw=(K, U16), iu=(K, U16), tm=(7 * K, FP), ow=(C, BF), z4=(C, HF), off=(Q, U16), olf=(C, FP),
    ss=(4 * (C + 2 * PAD), BF), qs=(512, X4), qss=(512, U8), ls=(3 * 128, X4), lss=(3 * 128, U8),
    ms=(512, BF), qm=(128, X4), qms=(128, U8), hs=(512, BF), qh=(128, X4), qhs=(128, U8),
    lh=(3 * Q + PAD, X4), lhs=(3 * Q + PAD, U8), sp=(4 * C, FP), ys=(C, FP))
SCRATCH = {n: ("sbuf", [128, w], d) for n, (w, d) in _SB.items()}
SCRATCH["ps"] = ("psum", [128, 8 * 512], FP)
SEMAPHORES = (["sv", "sa", "sp", "sg", "ldx", "ldz", "ldu", "ldw", "ldp", "sto", "stf"]
              + ["%s%d" % (n, t) for n in ("lS", "lH") for t in range(R)]
              + ["%s%d_%d" % (n, t, r) for n in ("aS", "aH") for t in range(R) for r in range(N)])


def _near(topo, a, b):
    ca, cb = topo.chip(a), topo.chip(b)
    return 2 if topo.mates(ca, cb) else 1 if topo.same_plane(ca, cb) else 0


def rank_program(g, core, T, topo):
    me = T.rank_of(core)
    if me is None:
        return
    cores = list(T.cores)

    def others(r):
        return [d for d in range(N) if d != r]

    def dests(r):
        return sorted(others(r), key=lambda d: (_near(topo, cores[r], cores[d]), d))

    def slot_s(r, d):
        return 128 * others(d).index(r)

    def slot_h(r, d):
        return Q * (2 - dests(d).index(r))

    eng = {"v": g.vector, "a": g.scalar, "p": g.tensor, "g": g, "y": g.sync}
    own = {"v": "sv", "a": "sa", "p": "sp", "g": "sg"}
    known = {q: {} for q in eng}
    count, writer, readers, group = {}, {}, {}, {}

    def wait(q, toks):
        for s, val, clock, _ in sorted(toks, key=lambda k: -k[1]):
            if known[q].get(s, 0) < val:
                eng[q].wait_ge(T.sem[s], val)
                known[q][s] = val
                for s2, v2 in clock.items():
                    known[q][s2] = max(known[q].get(s2, 0), v2)

    def before(q, r, w=(), x=()):
        toks = [writer[k] for k in list(r) + list(x) if k in writer]
        for k in w:
            toks += readers.get(k, [])
            if k in writer and not (q == "p" and writer[k][3] == "p"):
                toks.append(writer[k])
        for k in x:
            toks += [t for t in readers.get(k, []) if t[3] != q]
        wait(q, toks)

    def after(tok, r, w):
        for k in r:
            readers.setdefault(k, []).append(tok)
        for k in w:
            writer[k] = tok
            readers[k] = []

    def op(q, name, args, r=(), w=(), x=(), **kw):
        before(q, r, w, x)
        e = eng[q]
        call = {"copy": lambda: e.tensor_copy(*args), "tt": lambda: e.tensor_tensor(*args),
                "ts": lambda: e.tensor_scalar(*args), "scan": lambda: e.tensor_tensor_scan(*args),
                "set": lambda: e.memset(*args), "quant": lambda: e.quantize_mx(*args),
                "turn": lambda: e.transpose(*args),
                "act": lambda: e.activation(*args, **kw), "mm": lambda: e.matmul_mx(*args),
                "iota": lambda: e.iota(*args, **kw), "sel": lambda: e.affine_select(*args)}[name]
        s = own[q]
        call().then_inc(T.sem[s], 1)
        count[s] = count.get(s, 0) + 1
        after([s, count[s], dict(known[q]), q], list(r) + list(x), w)

    def shared(s, q, n, r, w=()):
        count[s] = count.get(s, 0) + n
        tok = group.setdefault(s, [s, 0, {}, "dma"])
        tok[1] = count[s]
        for s2, v2 in known[q].items():
            tok[2][s2] = max(tok[2].get(s2, 0), v2)
        after(tok, r, w)

    def dma(q, out, in_, s, r=(), w=()):
        before(q, r, w)
        eng[q].dma_start(out, in_).then_inc(T.sem[s], 16)
        shared(s, q, 16, r, w)

    def send(d, out, in_, far, near, key):
        rid, pid, _ = topo.addr(cores[d])
        before("g", [key])
        g.remote_dma(out, in_, T.sem[far], T.sem[near], pid, rid, topo.mask(core, cores[d]))
        shared(near, "g", len(topo.engines(core, cores[d])), [key])

    def arrive(s, n, w):
        count[s] = n
        after([s, n, {}, "far"], [], w)

    def bank(b, n, a=0):
        return T.ps[:, 512 * b + a:512 * b + a + n]

    def u8(v):
        return v.bitcast(dt.uint8)

    XK = ["x0", "x1", "x2", "x3", "x4"]
    XR = ["xr0", "xr1"]
    MK = ["ms0", "ms1", "ms2", "ms3"]
    flag = dict(allow_small_or_imprecise_dtypes=True)

    dma("a", T.us[:], T.u[:], "ldu", w=["us"])
    dma("y", T.xs[:, 1024:4 * C], T.x[:, 1024:4 * C], "ldx", w=["xt"])
    dma("y", T.xs[:, 0:512], T.x[:, 0:512], "ldz", w=["xr0"])
    dma("a", T.xs[:, 512:1024], T.x[:, 512:1024], "ldz", w=["xr1"])

    op("g", "iota", (T.pi[:, 0:1], [[0, 1]], 0, 1), w=["pi"])
    op("g", "iota", (T.uli[:], [[16, 8]], 0, 0), w=["uli"])
    op("g", "iota", (T.t16[:], [[0, K], [1, 16]], 0, 0), w=["t16"], **flag)
    op("g", "iota", (T.t5[:], [[0, K], [1, 5]], 0, 0), w=["t5"], **flag)
    op("g", "iota", (T.t2[:], [[0, 8], [1, 2]], 0, 0), w=["t2"], **flag)
    op("g", "iota", (T.t4[:], [[0, Q], [1, 4]], 0, 0), w=["t4"], **flag)
    op("g", "iota", (T.jr[:], [[1, C]], -H2, 0), w=["jr"], **flag)
    op("g", "iota", (T.base[:], [[16, K]], 16, 0), w=["base"], **flag)
    op("g", "iota", (T.base[:, VA:16], [[0, 16 - VA]], 128, 0), w=["base"], **flag)
    op("g", "iota", (T.base[:, 16:VZ], [[0, VZ - 16]], H2, 0), w=["base"], **flag)
    op("v", "set", (T.ones[:], 1.0), w=["ones"])
    op("v", "set", (T.zs[:], 0.0), w=["%s%d" % (n, k) for n in "lg" for k in range(K)] + ["ck", "pk0", "pk1"])
    op("v", "set", (T.dd[:], 0.0), w=["dz"])
    op("v", "ts", (T.pj[:, 0:1], T.pi[:, 0:1], 15, None, A.bitwise_and), r=["pi"], w=["pj0"])
    op("v", "ts", (T.pj[:, 1:2], T.pi[:, 0:1], 2, 3, A.logical_shift_right, A.bitwise_and), r=["pi"], w=["pj1"])
    op("v", "ts", (T.pj[:, 2:3], T.pi[:, 0:1], 3, None, A.bitwise_and), r=["pi"], w=["pj2"])
    op("v", "ts", (T.pj[:, 3:4], T.pi[:, 0:1], 4, 1, A.logical_shift_right, A.bitwise_and), r=["pi"], w=["pj3"])
    op("v", "copy", (T.ul[:], T.uli[:]), r=["uli"], w=["ul"])
    op("v", "copy", (T.pf[:, 0:4], T.pj[:, 0:4]), r=["pj0", "pj1", "pj2", "pj3"], w=["pf"])
    op("v", "copy", (T.cu[:, 0:8], T.dd[:, 0:8]), r=["dz"], w=["cz"])
    op("v", "copy", (T.cw[:, 0:4], T.dd[:, 0:4]), r=["dz"], w=["cy"])
    op("v", "ts", (T.cap[:], T.t16[:], T.pf[:, 0:1], -LOW, A.not_equal, A.mult), r=["t16", "pf"], w=["cap"])
    op("a", "act", (T.ms[:], T.ones[:], F.Copy), r=["ones"], w=MK, scale=0.0)
    op("a", "act", (T.keep[:], T.t16[:], F.Sign), r=["t16"], w=["keep"])
    op("a", "act", (T.rad[:], T.keep[:], F.Identity), r=["keep"], w=["rad"], scale=4 * LOW, bias=-4 * LOW)
    op("v", "ts", (T.pf[:, 4:5], T.pf[:, 1:2], -2048.0, T.pf[:, 2:3], A.mult, A.add), r=["pf"], w=["pf4"])
    op("v", "ts", (T.k1[:], T.t5[:], 1.0, -2.0, A.is_equal, A.mult), r=["t5"], w=["k1"])
    op("v", "ts", (T.k2[:], T.t5[:], 0.5, None, A.is_gt), r=["t5"], w=["k2"])
    op("v", "quant", (T.qu[:], T.qus[:], T.us[:]), r=["us"], w=["qu"])
    op("v", "ts", (T.pf[:, 5:6], T.pf[:, 4:5], float(2 * C + 3 * 2048), None, A.add), r=["pf4"], w=["pf5"])
    op("v", "copy", (T.qb[:, 0:128].bitcast(dt.uint32), T.qu[:, 0:128].bitcast(dt.uint32).indirect(T.ul[:, 0:8])),
       r=["qu", "ul"], w=["qb"])
    op("a", "act", (T.qbs[:, 0:128], T.qus[:, 0:128].indirect(T.ul[:, 0:8]), F.Copy), r=["qu", "ul"], w=["qbs"])
    for key, view in (("spad0", T.ss[:, 0:4 * PAD]), ("spad1", T.ss[:, 4 * (PAD + C):4 * (2 * PAD + C)]),
                      ("hpad", T.hs[:, 4 * Q:512])):
        op("a", "act", (view, T.ones[:, 0:4 * PAD], F.Copy), r=["ones"], w=[key], scale=0.0)
    op("a", "act", (T.jv[:], T.jr[:], F.Copy), r=["jr"], w=["jv"], scale=1.0 / 4096)
    for b in range(4):
        op("g", "sel", (T.es[:, 512 * b:512 * b + 512], T.ones[:], [[1, 512]], A.is_equal, 0.0, -b, -4),
           r=["ones"], w=["e%d" % b])
    wait("y", [writer["xr0"]])
    dma("y", u8(T.qw[:]), T.wc[:], "ldw", w=["qw"])
    dma("y", T.qws[:], T.ws[:], "ldw", w=["qw2"])
    dma("y", T.vs[:], T.v[:], "ldw", w=["vs"])

    order = dests(me) + [me]
    shift = [Q * (order.index(q) - q) for q in range(N)]
    top = C - 128
    QK = ["qx0", "qx1"]

    for t in range(R):
        op("v", "quant", (T.qx[:, top:C], T.qxs[:, top:C], T.xs[:, 4 * top:4 * C]), r=XK + ["xt"], w=["qx0"])
        op("p", "mm", (bank(2, C - top), T.qb[:], T.qbs[:], T.qx[:, top:C], T.qxs[:, top:C], True, True),
           r=["qb", "qbs", "qx0"], w=["b2"])
        span = {0: (top, C, 2), 1: (0, top, 0)}

        def mask(n):
            a, z, bk = span[n]
            op("v", "tt", (T.am[:, a:z], bank(bk, z - a), T.cap[:, a:z], A.add), r=["cap"], w=["am%d" % n],
               x=["b%d" % bk])

        def hold(n):
            a, z, bk = span[n]
            op("v", "scan", (T.zz[:, a:z], T.rad[:, a:z], T.am[:, a:z], 0.0, A.add, A.max),
               r=["rad", "am%d" % n], w=["z%d" % n])

        if t == 0:
            op("v", "quant", (T.qm[:], T.qms[:], T.ms[:]), r=MK, w=["qm"])
            op("v", "tt", (T.k5[:], T.k1[:], T.k2[:], A.add), r=["k1", "k2"], w=["k5"])
            for i in range(3):
                dma("y", u8(T.ls[:, 128 * i + Q:128 * i + 128]), u8(T.qm[:, 0:PAD]), "ldp", r=["qm"], w=["lpad%d" % i])
                dma("y", T.lss[:, 128 * i + Q:128 * i + 128], T.qms[:, 0:PAD], "ldp", r=["qm"], w=["lspad%d" % i])
            dma("y", u8(T.lh[:, 3 * Q:3 * Q + PAD]), u8(T.qm[:, 0:PAD]), "ldp", r=["qm"], w=["hp0"])
            dma("y", T.lhs[:, 3 * Q:3 * Q + PAD], T.qms[:, 0:PAD], "ldp", r=["qm"], w=["hp1"])
        op("v", "quant", (T.qx[:, 0:top], T.qxs[:, 0:top], T.xs[:, 0:4 * top]), r=XK + XR, w=["qx1"])
        for b in range(2):
            op("p", "mm", (bank(b, C), T.qb[:], T.qbs[:], T.qx[:], T.qxs[:], True, True),
               r=["qb", "qbs"] + QK, w=["b%d" % b])

        def flags(c, a, z):
            q = c // 8
            if q == 0:
                return T.fl[:, F0 + 128 * c + a:F0 + 128 * c + z]
            o = (F1 if q == 1 else 0) + c % 8
            return T.fl[:, o + 8 * a:o + 8 * (z - 1) + 1:8]

        def sign(c):
            e = 128 * (c // 8 + 1)
            op("a", "act", (flags(c, 0, e), bank(1, e), F.Sign), r=["z0" if 16 * c >= top else "z1"],
               w=["f%d" % c, "h%d" % c], x=["b1"], bias=T.zz[:, 16 * c + 15:16 * c + 16], scale=-1.0)

        def below(c):
            m = 16 * c + 16
            op("a", "act", (flags(c, 0, m), flags(c, 0, m), F.Relu), r=["f%d" % c], w=["f%d" % c, "l%d" % c],
               accum_out=T.zs[:, 5 * c:5 * c + 1])

        def above(c):
            m, e = 16 * c + 16, 128 * (c // 8 + 1)
            if m < e:
                op("a", "act", (flags(c, m, e), flags(c, m, e), F.Relu), r=["h%d" % c],
                   w=["h%d" % c, "g%d" % c], scale=-1.0, accum_out=T.zs[:, 5 * c + 2:5 * c + 3])

        def compare(c):
            m, e = 16 * c + 16, 128 * (c // 8 + 1)
            s, zk = T.zz[:, m - 1:m], "z0" if 16 * c >= top else "z1"
            op("v", "ts", (flags(c, 0, m), bank(0, m), s, None, A.is_lt), r=[zk], w=["f%d" % c], x=["b0"])
            if m < e:
                op("v", "ts", (flags(c, m, e), bank(0, e - m, m), s, None, A.is_le), r=[zk], w=["h%d" % c], x=["b0"])

        def total(c):
            h, z = 64 * (c // 8 + 1), H2 * (c - VA + 1)
            op("v", "scan", (T.rs[:, z - h:z], flags(c, 0, h), flags(c, h, 2 * h), float(-h), A.add, A.add),
               r=["f%d" % c, "h%d" % c], w=["r%d" % c])

        def place(a, z, keys):
            op("v", "copy", (T.ow[:, 0:C].indirect(T.iw[:, a:z]), T.jv[:, 16 * a:16 * z]), r=keys + ["jv"], w=["ow"])

        def fold(a, z, keys):
            op("v", "scan", (T.zo[:, 5 * a:5 * z], T.k5[:, 5 * a:5 * z], T.zs[:, 5 * a:5 * z], 0.0, A.mult, A.add),
               r=keys + ["ck", "k5"] + ["%s%d" % (n, k) for n in "lg" for k in range(a, z)], w=["rk%d" % a])

        def narrow(a, z):
            op("v", "copy", (T.iw[:, a:z], T.zo[:, 5 * a + 4:5 * z:5]), r=["rk%d" % a], w=["iw%d" % a])

        mask(0)
        if t == 0:
            op("v", "ts", (T.c4[:], T.t4[:], T.pf[:, 1:2], 0.125, A.is_le, A.subtract), r=["t4", "pf"], w=["c4"])
        hold(0)
        mask(1)
        compare(16)
        hold(1)
        sign(K - 1)
        for c in range(K - 1, VZ, -1):
            sign(c - 1)
            below(c)
            if c > VZ + 1:
                above(c)
        sign(VA - 1)
        below(VZ)
        above(VZ + 1)
        above(VZ)
        for c in range(VA - 1, -1, -1):
            if c > 0:
                sign(c - 1)
            below(c)
            above(c)
        rows = list(range(16, VZ)) + list(range(VA, 16))
        for i, c in enumerate(rows):
            if i + 1 < len(rows):
                compare(rows[i + 1])
            else:
                op("v", "tt", (T.eq[:], bank(0, C), T.zz[:], A.is_equal), r=["z0", "z1"], w=["eq"], x=["b0"])
            total(c)
        FK = ["f%d" % c for c in range(K)]
        op("v", "scan", (T.cw[:, 4:516], T.fl[:, 1024:2048:2], T.fl[:, 1025:2048:2], 0.0, A.add, A.add),
           r=FK[16:] + ["cy"], w=["cu1"])
        op("v", "scan", (T.cu[:, 8:1032], T.fl[:, 0:1024], T.fl[:, F1:F1 + 1024], 0.0, A.add, A.add),
           r=FK[8:] + ["cz"], w=["cu0"])
        op("v", "scan", (T.dd[:, 144:272], T.cw[:, 7:516:4], T.cw[:, 3:512:4], 0.0, A.max, A.subtract),
           r=["cu1", "dz"], w=["d1"])
        op("v", "scan", (T.dd[:, 16:144], T.cu[:, 15:1032:8], T.cu[:, 7:1024:8], 0.0, A.max, A.subtract),
           r=["cu0", "dz"], w=["d0"])
        op("v", "scan", (T.cr[:], T.keep[:], T.eq[:], 0.0, A.mult, A.subtract), r=["keep", "eq"], w=["cr"])
        op("v", "turn", (T.tr[:, 0:256], T.dd[:, 16:272]), r=["d0", "d1"], w=["t0"])
        op("v", "turn", (T.tr[:, 256:544], T.dd[:, 0:288]), r=["d0", "d1"], w=["t1"])
        op("v", "copy", (T.zs[:, 5 * VA:5 * VZ:5], T.rs[:, H2 - 1:H2 * (VZ - VA):H2]),
           r=["r%d" % k for k in range(VA, VZ)], w=["l%d" % k for k in range(VA, VZ)])
        op("v", "tt", (T.zs[:, 1:5 * K:5], T.cr[:, 15:C:16], T.base[:], A.add), r=["cr", "base"], w=["ck"])
        op("v", "scan", (T.su[:, 0:256], T.keep[:, 0:256], T.tr[:, 0:256], 0.0, A.mult, A.add), r=["t0"], w=["s0"])
        fold(16, K, [])
        op("v", "scan", (T.su[:, 256:528], T.keep[:, 0:272], T.tr[:, 256:528], 0.0, A.mult, A.add), r=["t1"], w=["s1"])
        if t == 0:
            op("v", "ts", (T.m0[:], T.t2[:], T.pf[:, 3:4], None, A.is_equal), r=["t2", "pf"], w=["m0"])
            op("v", "ts", (T.m1[:], T.t2[:], T.pf[:, 3:4], None, A.not_equal), r=["t2", "pf"], w=["m1"])
        op("v", "tt", (T.zs[:, 3:80:5], T.su[:, 15:256:16], T.m0[:], A.mult), r=["s0", "m0"], w=["pk0"])
        op("v", "tt", (T.zs[:, 4:80:5], T.su[:, 256 + 31:528:16], T.m1[:], A.mult), r=["s1", "m1"], w=["pk1"])
        narrow(16, K)
        fold(0, 16, ["pk0", "pk1"])
        place(16, K, ["iw16"])
        narrow(0, 16)
        IK = ["iw0", "iw16"]
        place(0, 16, IK)

        def lay(step, h):
            a, z = H2 * h, H2 * h + H2
            if step == 0:
                op("v", "scan", (T.z4[:, a:z], T.c4[:, a:z], T.ow[:, a:z], 0.0, A.add, A.min), r=["ow", "c4"],
                   w=["z4%d" % h])
            else:
                op("v", "ts", (T.off[:, a // 4:z // 4], T.z4[:, a + 3:z:4], 16384.0, T.pf[:, 5:6], A.mult, A.add),
                   r=["z4%d" % h, "pf5"], w=["off%d" % h])

        def gather(q, k):
            o, s, n = K * order[k], 4 * (PAD + Q * k), GV[k]
            keys = XK + XR + ["xt", "off%d" % (order[k] // 2)]
            if q == "v":
                op("v", "copy", (T.ss[:, s:s + 16 * n], T.xs[:, 0:4 * C].indirect(T.off[:, o:o + n])),
                   r=keys, w=["sv%d" % k])
            else:
                op("a", "act", (T.ss[:, s + 16 * n:s + 4 * Q], T.xs[:, 0:4 * C].indirect(T.off[:, o + n:o + K]), F.Copy),
                   r=keys, w=["sa%d" % k])

        def pack(k):
            s = 4 * Q * k + (4 * PAD if k == 3 else 0)
            edge = "spad0" if k == 0 else "spad1" if k == 3 else "sa%d" % (k - 1)
            op("v", "quant", (T.qs[:, 128 * k:128 * k + 128], T.qss[:, 128 * k:128 * k + 128], T.ss[:, s:s + 512]),
               r=["sv%d" % k, "sa%d" % k, edge], w=["qs%d" % k])

        lS, aS, lH = "lS%d" % t, "aS%d_%d" % (t, me), "lH%d" % t

        def leave(k):
            s, l = 128 * k + PAD, slot_s(me, order[k])
            pack(k)
            send(order[k], u8(T.ls[:, l:l + Q]), u8(T.qs[:, s:s + Q]), aS, lS, "qs%d" % k)
            send(order[k], T.lss[:, l:l + Q], T.qss[:, s:s + Q], aS, lS, "qs%d" % k)

        h = order[0] // 2
        lay(0, h)
        lay(0, 1 - h)
        lay(1, h)
        lay(1, 1 - h)
        for k in range(N):
            gather("a", k)
        for k in range(N - 1):
            gather("v", k)
            leave(k)
        gather("v", 3)
        pack(3)
        for r in others(me):
            arrive("aS%d_%d" % (t, r), 2 * len(topo.engines(cores[r], core)), ["ls%d" % r])

        if t == 0:
            op("v", "quant", (T.qe[:], T.qes[:], T.es[:]), r=["e0", "e1", "e2", "e3"], w=["qe"])
        tm = [T.tm[:, K * i:K * i + K] for i in range(7)]

        def slots():
            for q in range(1, N):
                op("v", "ts", (tm[q - 1], T.iw[:], float(Q * q), float(shift[q] - shift[q - 1]), A.is_ge, A.mult),
                   r=IK, w=["tm%d" % (q - 1)])
            op("v", "ts", (tm[3], T.iw[:], float(shift[0]), None, A.add), r=IK, w=["tm3"])
            op("v", "tt", (tm[4], tm[0], tm[1], A.add), r=["tm0", "tm1"], w=["tm4"])
            op("v", "tt", (tm[5], tm[2], tm[3], A.add), r=["tm2", "tm3"], w=["tm5"])
            op("v", "tt", (tm[6], tm[4], tm[5], A.add), r=["tm4", "tm5"], w=["tm6"])
            op("v", "copy", (T.iu[:], tm[6]), r=["tm6"], w=["iu"])

        if t > 0:
            slots()
        if t == R - 1:
            op("v", "ts", (T.olf[:], T.ow[:], 4096.0, float(H2), A.mult, A.add), r=["ow"], w=["olf"])
            dma("y", T.ol[:], T.olf[0:128:16, :], "sto", r=["olf"])

        def unpack(bk, b, n, codes, scales, keys, start=True, stop=True):
            op("p", "mm", (bank(bk, n), T.qe[:, 128 * b:128 * b + 128], T.qes[:, 128 * b:128 * b + 128], codes, scales,
                           start, stop), r=["qe"] + keys, w=["b%d" % bk])

        def term(b, r, start, stop):
            if r == me:
                unpack(b, b, 128, T.qs[:, 384:512], T.qss[:, 384:512], ["qs3"], start, stop)
            else:
                l = slot_s(r, me)
                unpack(b, b, 128, T.ls[:, l:l + 128], T.lss[:, l:l + 128],
                       ["ls%d" % r, "lpad%d" % (l // 128), "lspad%d" % (l // 128)], start, stop)

        seq = sorted(range(2), key=lambda r: -1 if r == me else dests(r).index(me)) + [2, 3]
        early = seq.index(order[2])
        for i in range(early):
            for b in range(4):
                term(b, seq[i], i == 0, False)
        for b in range(4):
            for i in range(early, N):
                term(b, seq[i], i == 0, i == N - 1)
            if b % 2 == 0:
                op("a", "act", (T.ms[:, b:4 * Q:4], bank(b, Q), F.Copy), w=[MK[b]], x=["b%d" % b], scale=0.25)
            else:
                op("v", "ts", (T.ms[:, b:4 * Q:4], bank(b, Q), 0.25, None, A.mult), w=[MK[b]], x=["b%d" % b])
        op("v", "quant", (T.qm[:], T.qms[:], T.ms[:]), r=MK, w=["qm"])

        for b in range(4):
            op("p", "mm", (bank(4 + b, 128), T.qw[:, 128 * b:128 * b + 128], T.qws[:, 128 * b:128 * b + 128],
                           T.qm[:], T.qms[:], True, True), r=["qw", "qw2", "qm"], w=["b%d" % (4 + b)])
            if b % 2 == 0:
                op("a", "act", (T.hs[:, b:4 * Q:4], bank(4 + b, Q), F.Relu), w=["hs%d" % b], x=["b%d" % (4 + b)], scale=0.0625)
            else:
                op("v", "ts", (T.hs[:, b:4 * Q:4], bank(4 + b, Q), 0.0, 0.0625, A.max, A.mult),
                   w=["hs%d" % b], x=["b%d" % (4 + b)])
        op("v", "quant", (T.qh[:], T.qhs[:], T.hs[:]), r=["hs0", "hs1", "hs2", "hs3", "hpad"], w=["qh"])

        aH = "aH%d_%d" % (t, me)
        for d in order[:3]:
            l = slot_h(me, d)
            send(d, u8(T.lh[:, l:l + Q]), u8(T.qh[:, 0:Q]), aH, lH, "qh")
            send(d, T.lhs[:, l:l + Q], T.qhs[:, 0:Q], aH, lH, "qh")
        for k, r in enumerate(order[:3]):
            arrive("aH%d_%d" % (t, r), 2 * len(topo.engines(cores[r], core)), ["lh%d" % k])

        def add(bk, b, k):
            s = 4 * (PAD + Q * k) + b
            op("v", "tt", (T.sp[:, C * b + Q * k:C * b + Q * (k + 1)], bank(bk, Q), T.ss[:, s:s + 4 * Q:4], A.add),
               r=["sv%d" % k, "sa%d" % k], w=["p%d_%d" % (k, b)], x=["b%d" % bk])

        def back(q, b, a, z, key):
            win = T.sp[:, C * b:C * b + C].indirect(T.iu[:, a:z])
            out, keys = T.xs[:, 64 * a + b:64 * z:4], ["p%d_%d" % (k, b) for k in range(4)] + ["iu"]
            if q == "a":
                op("a", "act", (out, win, F.Copy), r=keys, w=[key], scale=0.5)
            else:
                op("v", "ts", (out, win, 0.5, None, A.mult), r=keys, w=[key])

        for b in range(4):
            unpack(b, b, 128, T.qh[:], T.qhs[:], ["qh"])
            add(b, b, 3)
        if t == 0:
            slots()
            op("v", "quant", (T.qv[:], T.qvs[:], T.vs[:]), r=["vs"], w=["qv"])
        for k in range(3):
            l, first = Q * (2 - k), 4 * ((k + 1) % 2)
            for b in range(4):
                unpack(first + b, b, 128, T.lh[:, l:l + 128], T.lhs[:, l:l + 128], ["lh%d" % k, "hp0", "hp1"])
            for b in range(4):
                add(first + b, b, k)
                if k == 2 and b < 2:
                    back("a", b, 0, K, XK[b])
        back("v", 2, 0, K, XK[2])
        back("a", 3, BV, K, XK[4])
        back("v", 3, 0, BV, XK[3])

    for h in range(2):
        a, z = H2 * h, H2 * h + H2
        key = "qx0" if h == 0 else "qx2"
        op("v", "quant", (T.qx[:, a:z], T.qxs[:, a:z], T.xs[:, 4 * a:4 * z]), r=XK, w=QK if h == 0 else ["qx2"])
        op("p", "mm", (bank(h, H2), T.qv[:], T.qvs[:], T.qx[:, a:z], T.qxs[:, a:z], True, True),
           r=["qv", key], w=["b%d" % h])
        dma("y", T.oc[:, 4 * a:4 * z], u8(T.qx[:, a:z]), "stf", r=[key])
    QK = QK + ["qx2"]
    op("a", "act", (T.ys[:, 0:H2], bank(0, H2), F.Copy), w=["y0"], x=["b0"])
    op("v", "copy", (T.ys[:, H2:C], bank(1, H2)), w=["y1"], x=["b1"])
    dma("a", T.y[:, 0:H2], T.ys[:, 0:H2], "stf", r=["y0"])
    dma("a", T.y[:, H2:C], T.ys[:, H2:C], "stf", r=["y1"])
    for k in range(4):
        dma("a" if k == 3 else "y", T.osc[4 * k:4 * k + 4, :], T.qxs[32 * k:32 * k + 4, :], "stf", r=QK)
    for s in SEMAPHORES:
        if count.get(s, 0) > known["g"].get(s, 0):
            g.wait_ge(T.sem[s], count[s])
